import numpy as np
import ml_dtypes


def mxq(x, axis, fmt="e4m3"):
    dtype, down = {"e4m3": (ml_dtypes.float8_e4m3fn, 7), "e5m2": (ml_dtypes.float8_e5m2, 14)}[fmt]
    v = np.moveaxis(np.asarray(x, np.float32).astype(ml_dtypes.bfloat16).astype(np.float64), axis, -1)
    blocks = v.reshape(v.shape[:-1] + (-1, 32))
    amax = np.abs(blocks).max(-1, keepdims=True)
    byte = np.maximum(np.where(amax > 0, np.frexp(amax)[1] - 1 + 127, 0) - down, 1)
    scale = np.exp2(byte - 127.0)
    codes = (blocks / scale).astype(np.float32).astype(dtype).astype(np.float64)
    return np.moveaxis((codes * scale).reshape(v.shape), -1, axis)


WIDE = False


def mx_kscale(k):
    if not WIDE:
        return np.ones(k)
    levels = np.array([10, -10, 5, -5, 0])
    if k % 512:
        return np.exp2(np.random.permutation(np.resize(levels, k // 32))).repeat(32)
    a = np.empty((k // 512, 16))
    for p in range(k // 512):
        a[p, :8] = np.random.permutation(np.resize(levels, 8))
        for g in range(8):
            far = levels[np.abs(levels - a[p, g]) >= 10]
            a[p, g + 8] = far[np.random.randint(len(far))]
    return np.exp2(a.ravel()).repeat(32)


def f64(x):
    return np.asarray(x).astype(np.float64)


def striped(idx):
    return np.tile(idx.reshape(-1, 16).T, (8, 1)).astype(np.uint16)


def unstriped(offs):
    return offs[:16].T.reshape(-1).astype(np.int64)


E2M1 = np.array([0.0, 0.5, 1.0, 1.5, 2.0, 3.0, 4.0, 6.0, -0.0, -0.5, -1.0, -1.5, -2.0, -3.0, -4.0, -6.0])


def pack_weight(w, fmt):
    k, n = w.shape
    w = f64(np.asarray(w, np.float32).astype(ml_dtypes.bfloat16)).reshape(k // 32, 32, n)
    amax = np.abs(w).max(1)
    if fmt == "e4m3":
        byte = np.frexp(amax)[1] - 1 + 127 - 7
    else:
        mant, ex = np.frexp(amax / 6.0)
        byte = np.where(mant > 0.5, ex, ex - 1) + 127
    byte = np.clip(np.where(amax > 0, byte, 1), 1, 254)
    scaled = (w * np.exp2(127.0 - byte)[:, None, :]).reshape(k, n).astype(np.float32)
    by_word = np.ascontiguousarray(scaled.reshape(k // 512, 128, 4, n).transpose(0, 1, 3, 2))
    if fmt == "e4m3":
        words = by_word.astype(ml_dtypes.float8_e4m3fn).view(np.uint8)
    else:
        c = by_word.astype(ml_dtypes.float4_e2m1fn).view(np.uint8) & 0xF
        words = (c[..., 0::2] | (c[..., 1::2] << 4)).reshape(k // 512, 128, 2 * n)
    return np.ascontiguousarray(words), np.ascontiguousarray(byte.astype(np.uint8).reshape(k // 512, 16, n))


def unpack_weight(words, scales, fmt):
    g, _, n = scales.shape
    words = np.ascontiguousarray(words).reshape(g, 128, n, -1)
    if fmt == "e4m3":
        vals = words.view(ml_dtypes.float8_e4m3fn).astype(np.float64)
    else:
        nib = np.empty((g, 128, n, 4), np.uint8)
        nib[..., 0::2] = words & 0xF
        nib[..., 1::2] = words >> 4
        vals = E2M1[nib]
    vals = vals * np.repeat(np.exp2(scales.astype(np.float64) - 127.0), 8, axis=1)[..., None]
    return vals.transpose(0, 1, 3, 2).reshape(g * 512, n)


def gelu(v):
    return 0.5 * v * (1.0 + np.tanh(np.sqrt(2.0 / np.pi) * (v + 0.044715 * v**3)))


T, S, K, H, T2, P, N = 2048, 1024, 1024, 1024, 2048, 1024, 512

def setup_inputs():
    n = np.random.standard_normal
    s = mx_kscale(K)[:, None]
    u = mx_kscale(H)[:, None]
    tab_words, tab_scales = pack_weight(n((K, T)) * s, "e4m3")
    w4_words, w4_scales = pack_weight(n((K, H)) / s * u.T / np.sqrt(K), "e2m1")
    w8_words, w8_scales = pack_weight(n((H, N)) / u / np.sqrt(H), "e4m3")
    return {
        "tab_words": tab_words, "tab_scales": tab_scales,
        "offs": striped(np.random.permutation(T)[:S]),
        "w4_words": w4_words, "w4_scales": w4_scales,
        "wgs": np.exp(0.3 * n((128, S))).astype(np.float32),
        "offs2": striped(np.random.permutation(T2)[:S]),
        "offs3": striped(np.random.permutation(T2)[:P]),
        "ifm": (0.8 * n((H, P)) * u).astype(np.float32),
        "wv": (1.5 * n((H, N)) / u / np.sqrt(H)).astype(np.float32),
        "w8_words": w8_words, "w8_scales": w8_scales,
    }

def reference(tab_words, tab_scales, offs, w4_words, w4_scales, wgs, offs2, offs3, ifm, wv, w8_words, w8_scales):
    v = unpack_weight(tab_words, tab_scales, "e4m3")[:, unstriped(offs)]
    w4 = unpack_weight(w4_words, w4_scales, "e2m1")
    h = w4.T @ v
    page = np.zeros((H, T2))
    page[:, unstriped(offs2)] = np.tile(f64(wgs), (H // 128, 1)) * h
    x = page[:, unstriped(offs3)]
    z = mxq(x + f64(ifm), 0, "e4m3")
    yv = mxq(f64(wv), 0, "e4m3").T @ z
    w8 = unpack_weight(w8_words, w8_scales, "e4m3")
    yg = w8.T @ z
    return yv / (1.0 + np.exp(-yg))

@@ -1,0 +1,252 @@
+from contextlib import ExitStack
+
+import concourse.mybir as mybir
+from concourse.masks import make_identity
+
+T, S, K, H, T2, M, N = 2048, 1024, 1024, 1024, 2048, 1024, 512
+FLOPS = 2 * K * H * S + 2 * 2 * H * N * M
+
+F32 = mybir.dt.float32
+BF16 = mybir.dt.bfloat16
+I32 = mybir.dt.int32
+U32 = mybir.dt.uint32
+U16 = mybir.dt.uint16
+U8 = mybir.dt.uint8
+FP8X4 = mybir.dt.float8_e4m3fn_x4
+FP4X4 = mybir.dt.float4_e2m1fn_x4
+MULT = mybir.AluOpType.mult
+SIGMOID = mybir.ActivationFunctionType.Sigmoid
+
+P = 128
+PASSES = 2
+SLICES = H // P
+HALF = 512
+CHUNK = 256
+CHUNKS = M // CHUNK
+EARLY_PAIRS = 2
+FIRST = 2
+
+
+def tile_list_beam_slot_gating_kernel(
+    tc, tab_words, tab_scales, offs, w4_words, w4_scales, wgs, offs2, offs3, ifm, wv, w8_words, w8_scales, out
+):
+    nc = tc.nc
+    with ExitStack() as ctx:
+        keep = ctx.enter_context(tc.tile_pool(name="keep", bufs=1))
+        ring = ctx.enter_context(tc.tile_pool(name="ring", bufs=2))
+        psum = ctx.enter_context(tc.psum_pool(name="psum", bufs=2))
+
+        list1 = keep.tile([P, S // 16], U16, name="list1")
+        list2 = keep.tile([P, S // 16], U16, name="list2")
+        list3 = keep.tile([P, M // 16], U16, name="list3")
+        nc.sync.dma_start(list1[:], offs)
+        nc.sync.dma_start(list2[:], offs2)
+        nc.sync.dma_start(list3[:], offs3)
+
+        tab_s = keep.tile([P, T], U8, name="tab_s", tag="late", align_bytes=64)
+        nc.vector.memset(tab_s[:].bitcast(I32), 0)
+        for q in range(4):
+            nc.sync.dma_start(
+                tab_s[32 * q : 32 * q + 8, :].bitcast(I32), tab_scales[:, 4 * q : 4 * q + 4, :].bitcast(I32)
+            )
+        tab_w = []
+        for a in range(PASSES):
+            t = keep.tile([P, T], U32, name=f"tab_w{a}", tag=f"big{a}", align_bytes=64)
+            nc.sync.dma_start(t[:].bitcast(I32), tab_words[a].rearrange("p t i -> p (t i)").bitcast(I32))
+            tab_w.append(t)
+
+        w4_hbm = w4_words.rearrange("a p n -> p a n")
+        w4_first = keep.tile([P, PASSES, 2 * P * FIRST], U8, name="w4_first", align_bytes=64)
+        nc.sync.dma_start(w4_first[:].bitcast(I32), w4_hbm[:, :, 0 : 2 * P * FIRST].bitcast(I32))
+        wgs_sb = keep.tile([P, S], F32, name="wgs_sb")
+        nc.sync.dma_start(wgs_sb[:, 0:HALF], wgs[:, 0:HALF])
+        w4_s = keep.tile([P, PASSES, H], U8, name="w4_s", align_bytes=64)
+        nc.vector.memset(w4_s[:].rearrange("p a n -> p (a n)").bitcast(I32), 0)
+        for q in range(4):
+            nc.sync.dma_start(
+                w4_s[32 * q : 32 * q + 4, :, :].bitcast(I32),
+                w4_scales[:, 4 * q : 4 * q + 4, :].rearrange("a r n -> r a n").bitcast(I32),
+            )
+        v_s1 = keep.tile([P, S], U8, name="v_s1", align_bytes=64)
+        nc.vector.memset(v_s1[:].bitcast(I32), 0)
+
+        pages = []
+        for i in range(2):
+            pg = keep.tile([P, T2], F32, name=f"page{i}", align_bytes=64)
+            nc.vector.memset(pg[:], 0.0)
+            pages.append(pg)
+
+        ident = keep.tile([P, P], F32, name="ident")
+        make_identity(nc, ident[:])
+
+        v_s0 = keep.tile([P, S], U8, name="v_s0", align_bytes=64)
+        nc.vector.tensor_copy(v_s0[:], tab_s[:].indirect(list1[:]))
+        nc.scalar.dma_start(v_s1[0:112, :].bitcast(I32), v_s0[4:116, :].bitcast(I32))
+        v_s = [v_s0, v_s1]
+
+        nc.sync.dma_start(wgs_sb[:, HALF:S], wgs[:, HALF:S])
+        w4_rest = keep.tile([P, PASSES, 2 * (H - P * FIRST)], U8, name="w4_rest", align_bytes=64)
+        nc.sync.dma_start(w4_rest[:].bitcast(I32), w4_hbm[:, :, 2 * P * FIRST : 2 * H].bitcast(I32))
+
+        v_w = {}
+        for a, jh in ((0, 0), (0, 1), (1, 0), (1, 1)):
+            t = keep.tile([P, HALF], U32, name=f"v_w{a}{jh}", tag=f"vw{a}{jh}", align_bytes=64)
+            nc.vector.tensor_copy(t[:], tab_w[a][:].indirect(list1[:, 32 * jh : 32 * jh + 32]))
+            v_w[(a, jh)] = t
+
+        late = keep.tile([P, SLICES + 4, M], F32, name="late", tag="late", align_bytes=64)
+        for k in range(SLICES // 2):
+            nc.sync.dma_start(
+                late[:, 2 * k : 2 * k + 2, :], ifm[256 * k : 256 * (k + 1), :].rearrange("(s p) m -> p s m", s=2)
+            )
+        wv_raw = late[:, SLICES : SLICES + 4, :].rearrange("p (a x) m -> p a (x m)", a=2)
+        nc.sync.dma_start(wv_raw, wv.rearrange("(a p j) n -> p a (j n)", a=2, j=4))
+        w8_w = keep.tile([P, PASSES, N], U32, name="w8_w", align_bytes=64)
+        nc.sync.dma_start(w8_w[:].bitcast(I32), w8_words.rearrange("a p n i -> p a (n i)").bitcast(I32))
+
+        for a in range(PASSES):
+            pg = keep.tile([P, T2], F32, name=f"page{2 + a}", tag=f"big{a}", align_bytes=64)
+            nc.gpsimd.memset(pg[:], 0.0)
+            pages.append(pg)
+
+        h = [keep.tile([P, S], F32, name=f"h{s}", tag=f"h{s}", align_bytes=64) for s in range(SLICES)]
+
+        def first_product(s, jh):
+            bank = psum.tile([P, HALF], F32, name="bank", tag="mm", bufs=4)
+            w4 = w4_first if s < FIRST else w4_rest
+            c0 = 2 * P * (s if s < FIRST else s - FIRST)
+            for a in range(PASSES):
+                nc.tensor.matmul_mx(
+                    out=bank[:],
+                    lhsT=w4[:, a, c0 : c0 + 2 * P].bitcast(FP4X4),
+                    lhsT_scale=w4_s[:, a, s * P : (s + 1) * P],
+                    rhs=v_w[(a, jh)][:].bitcast(FP8X4),
+                    rhs_scale=v_s[a][:, jh * HALF : (jh + 1) * HALF],
+                    start=(a == 0),
+                    stop=(a == PASSES - 1),
+                )
+            nc.scalar.copy(h[s][:, jh * HALF : (jh + 1) * HALF], bank[:])
+
+        for jh in range(2):
+            for s in range(FIRST):
+                first_product(s, jh)
+        for s in range(FIRST, SLICES):
+            for jh in range(2):
+                first_product(s, jh)
+
+        for q in range(4):
+            nc.sync.dma_start(
+                w4_s[32 * q + 4 : 32 * q + 8, :, 0:N].bitcast(I32),
+                w8_scales[:, 4 * q : 4 * q + 4, :].rearrange("a r n -> r a n").bitcast(I32),
+            )
+
+        wv_bf = keep.tile([P, PASSES, N, 4], BF16, name="wv_bf", align_bytes=64)
+        for a in range(PASSES):
+            nc.scalar.copy(wv_bf[:, a, :, :], wv_raw[:, a, :].rearrange("p (j n) -> p n j", j=4))
+        wv_w = keep.tile([P, PASSES, N], U32, name="wv_w", align_bytes=64)
+        wv_s = keep.tile([P, PASSES, N], U8, name="wv_s", align_bytes=64)
+
+        def page_of(s):
+            return pages[s % 2 + (2 if s >= SLICES - 2 else 0)]
+
+        def scatter(s, lo, hi):
+            nc.vector.tensor_tensor(
+                page_of(s)[:].indirect(list2[:, lo // 16 : hi // 16]), h[s][:, lo:hi], wgs_sb[:, lo:hi], MULT
+            )
+
+        zt = {}
+
+        def turn_and_add(k, c, x_of):
+            g, j = divmod(k, 2)
+            bank = psum.tile([P, 2, 2, P], F32, name="zt_bank", tag="a", bufs=2)
+            steps = [(True, b, i) for b in range(2) for i in range(2)] + [
+                (False, b, i) for b in range(2) for i in range(2)
+            ]
+            for n, (is_ifm, b, i) in enumerate(steps):
+                m0 = c * CHUNK + b * P
+                src = late[:, 2 * k + i, m0 : m0 + P] if is_ifm else x_of(i, b)
+                nc.tensor.matmul(
+                    bank[:, b, i, :], src, ident[:], start=(n == 0), stop=(n == len(steps) - 1), is_transpose=True
+                )
+            if j == 0:
+                zt[(g, c)] = ring.tile([P, 2, 2, P, 2], BF16, name="zt", tag="zt", bufs=4, align_bytes=64)
+            nc.scalar.copy(
+                zt[(g, c)][:, :, :, 64 * j : 64 * (j + 1), :],
+                bank[:].rearrange("m b i r -> m b (i r)").rearrange("m b (p u e) -> m b u p e", u=2, e=2),
+            )
+
+        def turn_back(g, c, dst):
+            bank = psum.tile([P, 2, 2, P], F32, name="z_bank", tag="b", bufs=2)
+            words = zt[(g, c)][:].rearrange("m b u p e -> m (b u p e)").bitcast(F32)
+            for b in range(2):
+                for u in range(2):
+                    w0 = (2 * b + u) * P
+                    nc.tensor.transpose(bank[:, b, u, :], words[:, w0 : w0 + P], ident[:])
+            nc.scalar.copy(dst.rearrange("p (b m u) -> p b m u", b=2, u=2), bank[:].rearrange("p b u m -> p b m u"))
+
+        z0_in = keep.tile([P, 2 * M], F32, name="z0_in", tag="z0_in", align_bytes=64)
+        z0_w = keep.tile([P, M], U32, name="z0_w", align_bytes=64)
+        z0_s = keep.tile([P, M], U8, name="z0_s", align_bytes=64)
+
+        for k in range(SLICES // 2):
+            if k == 0:
+                for jh in range(2):
+                    for s in range(2):
+                        scatter(s, jh * HALF, (jh + 1) * HALF)
+            else:
+                scatter(2 * k, 0, S)
+                scatter(2 * k + 1, 0, S)
+            if k < EARLY_PAIRS:
+                xs = []
+                for i in range(2):
+                    x = ring.tile([P, M], F32, name="x", tag="x", bufs=4)
+                    nc.vector.tensor_copy(x[:], page_of(2 * k + i)[:].indirect(list3[:]))
+                    xs.append(x)
+                for c in range(CHUNKS):
+                    turn_and_add(k, c, lambda i, b: xs[i][:, c * CHUNK + b * P : c * CHUNK + (b + 1) * P])
+                    if k == 1:
+                        turn_back(0, c, z0_in[:, 2 * c * CHUNK : 2 * (c + 1) * CHUNK])
+
+        nc.vector.quantize_mx(out=z0_w[:].bitcast(FP8X4), scales=z0_s[:], in_=z0_in[:].bitcast(BF16))
+        nc.vector.quantize_mx(
+            out=wv_w[:].rearrange("p a n -> p (a n)").bitcast(FP8X4),
+            scales=wv_s[:].rearrange("p a n -> p (a n)"),
+            in_=wv_bf[:].rearrange("p a n j -> p (a n j)"),
+        )
+
+        for c in range(CHUNKS):
+            cols = slice(c * CHUNK, (c + 1) * CHUNK)
+            xc = keep.tile([P, 4, CHUNK], F32, name=f"xc{c}", tag=("h7", "z0_in", "z1_in0", "gate01")[c], align_bytes=64)
+            for i in range(4):
+                nc.vector.tensor_copy(xc[:, i, :], page_of(4 + i)[:].indirect(list3[:, 16 * c : 16 * (c + 1)]))
+            for k in range(EARLY_PAIRS, SLICES // 2):
+                turn_and_add(k, c, lambda i, b: xc[:, 2 * (k - 2) + i, b * P : (b + 1) * P])
+            z1_in = keep.tile([P, 2 * CHUNK], F32, name=f"z1_in{c}", tag=f"z1_in{c}", align_bytes=64)
+            turn_back(1, c, z1_in[:])
+            z1_w = ring.tile([P, CHUNK], U32, name="z1_w", tag="z1_w", bufs=2, align_bytes=64)
+            z1_s = ring.tile([P, CHUNK], U8, name="z1_s", tag="z1_s", bufs=2, align_bytes=64)
+            nc.vector.quantize_mx(out=z1_w[:].bitcast(FP8X4), scales=z1_s[:], in_=z1_in[:].bitcast(BF16))
+            z_ops = [(z0_w[:, cols], z0_s[:, cols]), (z1_w[:], z1_s[:])]
+
+            for q in range(2):
+                banks = []
+                for w_w, w_s, row in ((w8_w, w4_s, 4), (wv_w, wv_s, 0)):
+                    bank = psum.tile([P, 2, CHUNK], F32, name="bank", tag="mm", bufs=4)
+                    for a in range(PASSES):
+                        for i in range(2):
+                            n0 = (2 * q + i) * P
+                            nc.tensor.matmul_mx(
+                                out=bank[:, i, :],
+                                lhsT=w_w[:, a, n0 : n0 + P].bitcast(FP8X4),
+                                lhsT_scale=w_s[row:P, a, n0 : n0 + P],
+                                rhs=z_ops[a][0].bitcast(FP8X4),
+                                rhs_scale=z_ops[a][1],
+                                start=(a == 0 and i == 0),
+                                stop=(a == PASSES - 1 and i == 1),
+                            )
+                    banks.append(bank)
+                gate = keep.tile([P, 2, CHUNK], F32, name=f"gate{c}{q}", tag=f"gate{c}{q}", align_bytes=64)
+                nc.scalar.activation(gate[:], banks[0][:], SIGMOID)
+                res = ring.tile([P, 2, CHUNK], F32, name="res", tag="res", bufs=4)
+                nc.vector.tensor_tensor(res[:], banks[1][:], gate[:], MULT)
+                nc.sync.dma_start(out[256 * q : 256 * (q + 1), cols].rearrange("(i p) m -> p i m", i=2), res[:])

@@ -23,7 +23,7 @@ SLICES = H // P
 HALF = 512
 CHUNK = 256
 CHUNKS = M // CHUNK
-EARLY_PAIRS = 2
+EARLY_PAIRS = 3
 FIRST = 2
 
 
@@ -34,7 +34,7 @@ def tile_list_beam_slot_gating_kernel(
     with ExitStack() as ctx:
         keep = ctx.enter_context(tc.tile_pool(name="keep", bufs=1))
         ring = ctx.enter_context(tc.tile_pool(name="ring", bufs=2))
-        psum = ctx.enter_context(tc.psum_pool(name="psum", bufs=2))
+        psum = ctx.enter_context(tc.psum_pool(name="psum", bufs=1))
 
         list1 = keep.tile([P, S // 16], U16, name="list1")
         list2 = keep.tile([P, S // 16], U16, name="list2")
@@ -44,7 +44,7 @@ def tile_list_beam_slot_gating_kernel(
         nc.sync.dma_start(list3[:], offs3)
 
         tab_s = keep.tile([P, T], U8, name="tab_s", tag="late", align_bytes=64)
-        nc.vector.memset(tab_s[:].bitcast(I32), 0)
+        nc.gpsimd.memset(tab_s[:].bitcast(I32), 0)
         for q in range(4):
             nc.sync.dma_start(
                 tab_s[32 * q : 32 * q + 8, :].bitcast(I32), tab_scales[:, 4 * q : 4 * q + 4, :].bitcast(I32)
@@ -58,8 +58,6 @@ def tile_list_beam_slot_gating_kernel(
         w4_hbm = w4_words.rearrange("a p n -> p a n")
         w4_first = keep.tile([P, PASSES, 2 * P * FIRST], U8, name="w4_first", align_bytes=64)
         nc.sync.dma_start(w4_first[:].bitcast(I32), w4_hbm[:, :, 0 : 2 * P * FIRST].bitcast(I32))
-        wgs_sb = keep.tile([P, S], F32, name="wgs_sb")
-        nc.sync.dma_start(wgs_sb[:, 0:HALF], wgs[:, 0:HALF])
         w4_s = keep.tile([P, PASSES, H], U8, name="w4_s", align_bytes=64)
         nc.vector.memset(w4_s[:].rearrange("p a n -> p (a n)").bitcast(I32), 0)
         for q in range(4):
@@ -70,23 +68,14 @@ def tile_list_beam_slot_gating_kernel(
         v_s1 = keep.tile([P, S], U8, name="v_s1", align_bytes=64)
         nc.vector.memset(v_s1[:].bitcast(I32), 0)
 
-        pages = []
-        for i in range(2):
-            pg = keep.tile([P, T2], F32, name=f"page{i}", align_bytes=64)
-            nc.vector.memset(pg[:], 0.0)
-            pages.append(pg)
-
-        ident = keep.tile([P, P], F32, name="ident")
-        make_identity(nc, ident[:])
+        page0 = keep.tile([P, T2], F32, name="page0", align_bytes=64)
+        nc.vector.memset(page0[:].bitcast(I32), 0)
 
         v_s0 = keep.tile([P, S], U8, name="v_s0", align_bytes=64)
         nc.vector.tensor_copy(v_s0[:], tab_s[:].indirect(list1[:]))
         nc.scalar.dma_start(v_s1[0:112, :].bitcast(I32), v_s0[4:116, :].bitcast(I32))
         v_s = [v_s0, v_s1]
 
-        nc.sync.dma_start(wgs_sb[:, HALF:S], wgs[:, HALF:S])
-        w4_rest = keep.tile([P, PASSES, 2 * (H - P * FIRST)], U8, name="w4_rest", align_bytes=64)
-        nc.sync.dma_start(w4_rest[:].bitcast(I32), w4_hbm[:, :, 2 * P * FIRST : 2 * H].bitcast(I32))
 
         v_w = {}
         for a, jh in ((0, 0), (0, 1), (1, 0), (1, 1)):
@@ -94,25 +83,31 @@ def tile_list_beam_slot_gating_kernel(
             nc.vector.tensor_copy(t[:], tab_w[a][:].indirect(list1[:, 32 * jh : 32 * jh + 32]))
             v_w[(a, jh)] = t
 
-        late = keep.tile([P, SLICES + 4, M], F32, name="late", tag="late", align_bytes=64)
+        page1 = keep.tile([P, T2], F32, name="page1", tag="big1", align_bytes=64)
+        nc.vector.memset(page1[:].bitcast(I32), 0)
+        pages = [page0, page1]
+
+        ident = keep.tile([P, P], F32, name="ident")
+        make_identity(nc, ident[:])
+
+        late = keep.tile([P, SLICES + 5, M], F32, name="late", tag="late", align_bytes=64)
+        wgs_sb = late[:, SLICES + 4, :]
+        for jh in range(2):
+            nc.sync.dma_start(wgs_sb[:, jh * HALF : (jh + 1) * HALF], wgs[:, jh * HALF : (jh + 1) * HALF])
+        w4_rest = keep.tile([P, PASSES, 2 * (H - P * FIRST)], U8, name="w4_rest", tag="big0", align_bytes=64)
+        nc.sync.dma_start(w4_rest[:].bitcast(I32), w4_hbm[:, :, 2 * P * FIRST : 2 * H].bitcast(I32))
+        wv_raw = late[:, SLICES : SLICES + 4, :].rearrange("p (a x) m -> p a (x m)", a=2)
         for k in range(SLICES // 2):
             nc.sync.dma_start(
                 late[:, 2 * k : 2 * k + 2, :], ifm[256 * k : 256 * (k + 1), :].rearrange("(s p) m -> p s m", s=2)
             )
-        wv_raw = late[:, SLICES : SLICES + 4, :].rearrange("p (a x) m -> p a (x m)", a=2)
-        nc.sync.dma_start(wv_raw, wv.rearrange("(a p j) n -> p a (j n)", a=2, j=4))
-        w8_w = keep.tile([P, PASSES, N], U32, name="w8_w", align_bytes=64)
-        nc.sync.dma_start(w8_w[:].bitcast(I32), w8_words.rearrange("a p n i -> p a (n i)").bitcast(I32))
-
-        for a in range(PASSES):
-            pg = keep.tile([P, T2], F32, name=f"page{2 + a}", tag=f"big{a}", align_bytes=64)
-            nc.gpsimd.memset(pg[:], 0.0)
-            pages.append(pg)
+            if k == 1:
+                nc.sync.dma_start(wv_raw, wv.rearrange("(a p j) n -> p a (j n)", a=2, j=4))
 
         h = [keep.tile([P, S], F32, name=f"h{s}", tag=f"h{s}", align_bytes=64) for s in range(SLICES)]
 
         def first_product(s, jh):
-            bank = psum.tile([P, HALF], F32, name="bank", tag="mm", bufs=4)
+            bank = psum.tile([P, HALF], F32, name="h_bank", tag=f"bank{2 * jh + s % 2}")
             w4 = w4_first if s < FIRST else w4_rest
             c0 = 2 * P * (s if s < FIRST else s - FIRST)
             for a in range(PASSES):
@@ -134,20 +129,25 @@ def tile_list_beam_slot_gating_kernel(
             for jh in range(2):
                 first_product(s, jh)
 
+        w8_w = keep.tile([P, PASSES, N], U32, name="w8_w", tag="vw00", align_bytes=64)
+        nc.sync.dma_start(w8_w[:].bitcast(I32), w8_words.rearrange("a p n i -> p a (n i)").bitcast(I32))
+
         for q in range(4):
             nc.sync.dma_start(
                 w4_s[32 * q + 4 : 32 * q + 8, :, 0:N].bitcast(I32),
                 w8_scales[:, 4 * q : 4 * q + 4, :].rearrange("a r n -> r a n").bitcast(I32),
             )
 
-        wv_bf = keep.tile([P, PASSES, N, 4], BF16, name="wv_bf", align_bytes=64)
+        q_in = keep.tile([P, 4 * M], F32, name="q_in", tag="q_in", align_bytes=64)
+        z0_in = q_in[:, 0 : 2 * M]
+        wv_flat = q_in[:, 2 * M : 4 * M].bitcast(BF16)
+        wv_bf = wv_flat.rearrange("p (a n j) -> p a n j", a=2, j=4)
         for a in range(PASSES):
             nc.scalar.copy(wv_bf[:, a, :, :], wv_raw[:, a, :].rearrange("p (j n) -> p n j", j=4))
-        wv_w = keep.tile([P, PASSES, N], U32, name="wv_w", align_bytes=64)
         wv_s = keep.tile([P, PASSES, N], U8, name="wv_s", align_bytes=64)
 
         def page_of(s):
-            return pages[s % 2 + (2 if s >= SLICES - 2 else 0)]
+            return pages[s % 2]
 
         def scatter(s, lo, hi):
             nc.vector.tensor_tensor(
@@ -158,7 +158,7 @@ def tile_list_beam_slot_gating_kernel(
 
         def turn_and_add(k, c, x_of):
             g, j = divmod(k, 2)
-            bank = psum.tile([P, 2, 2, P], F32, name="zt_bank", tag="a", bufs=2)
+            bank = psum.tile([P, 2, 2, P], F32, name="zt_bank", tag=f"bank{4 + c}")
             steps = [(True, b, i) for b in range(2) for i in range(2)] + [
                 (False, b, i) for b in range(2) for i in range(2)
             ]
@@ -169,14 +169,14 @@ def tile_list_beam_slot_gating_kernel(
                     bank[:, b, i, :], src, ident[:], start=(n == 0), stop=(n == len(steps) - 1), is_transpose=True
                 )
             if j == 0:
-                zt[(g, c)] = ring.tile([P, 2, 2, P, 2], BF16, name="zt", tag="zt", bufs=4, align_bytes=64)
+                zt[(g, c)] = ring.tile([P, 2, 2, P, 2], BF16, name="zt", tag="zt", bufs=8, align_bytes=64)
             nc.scalar.copy(
                 zt[(g, c)][:, :, :, 64 * j : 64 * (j + 1), :],
                 bank[:].rearrange("m b i r -> m b (i r)").rearrange("m b (p u e) -> m b u p e", u=2, e=2),
             )
 
         def turn_back(g, c, dst):
-            bank = psum.tile([P, 2, 2, P], F32, name="z_bank", tag="b", bufs=2)
+            bank = psum.tile([P, 2, 2, P], F32, name="z_bank", tag=f"bank{4 + c}")
             words = zt[(g, c)][:].rearrange("m b u p e -> m (b u p e)").bitcast(F32)
             for b in range(2):
                 for u in range(2):
@@ -184,8 +184,6 @@ def tile_list_beam_slot_gating_kernel(
                     nc.tensor.transpose(bank[:, b, u, :], words[:, w0 : w0 + P], ident[:])
             nc.scalar.copy(dst.rearrange("p (b m u) -> p b m u", b=2, u=2), bank[:].rearrange("p b u m -> p b m u"))
 
-        z0_in = keep.tile([P, 2 * M], F32, name="z0_in", tag="z0_in", align_bytes=64)
-        z0_w = keep.tile([P, M], U32, name="z0_w", align_bytes=64)
         z0_s = keep.tile([P, M], U8, name="z0_s", align_bytes=64)
 
         for k in range(SLICES // 2):
@@ -199,7 +197,7 @@ def tile_list_beam_slot_gating_kernel(
             if k < EARLY_PAIRS:
                 xs = []
                 for i in range(2):
-                    x = ring.tile([P, M], F32, name="x", tag="x", bufs=4)
+                    x = ring.tile([P, M], F32, name="x", tag="x", bufs=6)
                     nc.vector.tensor_copy(x[:], page_of(2 * k + i)[:].indirect(list3[:]))
                     xs.append(x)
                 for c in range(CHUNKS):
@@ -207,46 +205,81 @@ def tile_list_beam_slot_gating_kernel(
                     if k == 1:
                         turn_back(0, c, z0_in[:, 2 * c * CHUNK : 2 * (c + 1) * CHUNK])
 
-        nc.vector.quantize_mx(out=z0_w[:].bitcast(FP8X4), scales=z0_s[:], in_=z0_in[:].bitcast(BF16))
+        wv_w = keep.tile([P, PASSES, N], U32, name="wv_w", tag="h6", align_bytes=64)
+        z0_w = keep.tile([P, M], U32, name="z0_w", tag="h7", align_bytes=64)
+        xc = []
+
+        def late_gathers(c, tile):
+            for i in range(2):
+                nc.vector.tensor_copy(tile[:, i, :], pages[i][:].indirect(list3[:, 16 * c : 16 * (c + 1)]))
+            xc.append(tile)
+
+        xc_first = keep.tile([P, 2, 2, CHUNK], F32, name="xc_first", align_bytes=64)
+        for c in range(2):
+            late_gathers(c, xc_first[:, c, :, :])
+        nc.vector.quantize_mx(out=z0_w[:].bitcast(FP8X4), scales=z0_s[:], in_=z0_in.bitcast(BF16))
         nc.vector.quantize_mx(
             out=wv_w[:].rearrange("p a n -> p (a n)").bitcast(FP8X4),
             scales=wv_s[:].rearrange("p a n -> p (a n)"),
-            in_=wv_bf[:].rearrange("p a n j -> p (a n j)"),
+            in_=wv_flat,
         )
+        z1 = []
 
-        for c in range(CHUNKS):
-            cols = slice(c * CHUNK, (c + 1) * CHUNK)
-            xc = keep.tile([P, 4, CHUNK], F32, name=f"xc{c}", tag=("h7", "z0_in", "z1_in0", "gate01")[c], align_bytes=64)
-            for i in range(4):
-                nc.vector.tensor_copy(xc[:, i, :], page_of(4 + i)[:].indirect(list3[:, 16 * c : 16 * (c + 1)]))
-            for k in range(EARLY_PAIRS, SLICES // 2):
-                turn_and_add(k, c, lambda i, b: xc[:, 2 * (k - 2) + i, b * P : (b + 1) * P])
+        def finish_z(c):
+            turn_and_add(EARLY_PAIRS, c, lambda i, b: xc[c][:, i, b * P : (b + 1) * P])
             z1_in = keep.tile([P, 2 * CHUNK], F32, name=f"z1_in{c}", tag=f"z1_in{c}", align_bytes=64)
             turn_back(1, c, z1_in[:])
-            z1_w = ring.tile([P, CHUNK], U32, name="z1_w", tag="z1_w", bufs=2, align_bytes=64)
-            z1_s = ring.tile([P, CHUNK], U8, name="z1_s", tag="z1_s", bufs=2, align_bytes=64)
+            z1_w = ring.tile([P, CHUNK], U32, name="z1_w", tag="z1_w", bufs=4, align_bytes=64)
+            z1_s = ring.tile([P, CHUNK], U8, name="z1_s", tag="z1_s", bufs=4, align_bytes=64)
             nc.vector.quantize_mx(out=z1_w[:].bitcast(FP8X4), scales=z1_s[:], in_=z1_in[:].bitcast(BF16))
-            z_ops = [(z0_w[:, cols], z0_s[:, cols]), (z1_w[:], z1_s[:])]
+            z1.append((z1_w, z1_s))
 
+        y_banks = {}
+
+        def second_pass(c, q, w, a):
+            cols = slice(c * CHUNK, (c + 1) * CHUNK)
+            if a == 0:
+                y_banks[(c, q, w)] = psum.tile([P, 2, CHUNK], F32, name="y_bank", tag=f"bank{4 * (c % 2) + 2 * q + w}")
+                z_w, z_s = z0_w[:, cols], z0_s[:, cols]
+            else:
+                z_w, z_s = z1[c][0][:], z1[c][1][:]
+            w_w, w_s, row = ((w8_w, w4_s, 4), (wv_w, wv_s, 0))[w]
+            for i in range(2):
+                n0 = (2 * q + i) * P
+                nc.tensor.matmul_mx(
+                    out=y_banks[(c, q, w)][:, i, :],
+                    lhsT=w_w[:, a, n0 : n0 + P].bitcast(FP8X4),
+                    lhsT_scale=w_s[row:P, a, n0 : n0 + P],
+                    rhs=z_w.bitcast(FP8X4),
+                    rhs_scale=z_s,
+                    start=(a == 0 and i == 0),
+                    stop=(a == PASSES - 1 and i == 1),
+                )
+
+        def gate_and_store(c, q):
+            cols = slice(c * CHUNK, (c + 1) * CHUNK)
+            logit, resp = y_banks[(c, q, 0)], y_banks[(c, q, 1)]
+            gate = ring.tile([P, 2, CHUNK], F32, name="gate", tag="gate", bufs=4)
+            nc.scalar.activation(gate[:], logit[:], SIGMOID)
+            res = ring.tile([P, 2, CHUNK], F32, name="res", tag="res", bufs=4)
+            nc.vector.tensor_tensor(res[:], resp[:], gate[:], MULT)
+            nc.sync.dma_start(out[256 * q : 256 * (q + 1), cols].rearrange("(i p) m -> p i m", i=2), res[:])
+
+        xc_rest = keep.tile([P, 2, 2, CHUNK], F32, name="xc_rest", tag="q_in", align_bytes=64)
+        for c in range(2, CHUNKS):
+            late_gathers(c, xc_rest[:, c - 2, :, :])
+        finish_z(0)
+        finish_z(1)
+        for w in range(2):
             for q in range(2):
-                banks = []
-                for w_w, w_s, row in ((w8_w, w4_s, 4), (wv_w, wv_s, 0)):
-                    bank = psum.tile([P, 2, CHUNK], F32, name="bank", tag="mm", bufs=4)
-                    for a in range(PASSES):
-                        for i in range(2):
-                            n0 = (2 * q + i) * P
-                            nc.tensor.matmul_mx(
-                                out=bank[:, i, :],
-                                lhsT=w_w[:, a, n0 : n0 + P].bitcast(FP8X4),
-                                lhsT_scale=w_s[row:P, a, n0 : n0 + P],
-                                rhs=z_ops[a][0].bitcast(FP8X4),
-                                rhs_scale=z_ops[a][1],
-                                start=(a == 0 and i == 0),
-                                stop=(a == PASSES - 1 and i == 1),
-                            )
-                    banks.append(bank)
-                gate = keep.tile([P, 2, CHUNK], F32, name=f"gate{c}{q}", tag=f"gate{c}{q}", align_bytes=64)
-                nc.scalar.activation(gate[:], banks[0][:], SIGMOID)
-                res = ring.tile([P, 2, CHUNK], F32, name="res", tag="res", bufs=4)
-                nc.vector.tensor_tensor(res[:], banks[1][:], gate[:], MULT)
-                nc.sync.dma_start(out[256 * q : 256 * (q + 1), cols].rearrange("(i p) m -> p i m", i=2), res[:])
+                second_pass(0, q, w, 0)
+        for c in range(CHUNKS):
+            if c == 1:
+                finish_z(2)
+                finish_z(3)
+            for q in range(2):
+                for w in range(2):
+                    if c > 0:
+                        second_pass(c, q, w, 0)
+                    second_pass(c, q, w, 1)
+                gate_and_store(c, q)

@@ -97,7 +97,7 @@ def tile_list_beam_slot_gating_kernel(
         w4_rest = keep.tile([P, PASSES, 2 * (H - P * FIRST)], U8, name="w4_rest", tag="big0", align_bytes=64)
         nc.sync.dma_start(w4_rest[:].bitcast(I32), w4_hbm[:, :, 2 * P * FIRST : 2 * H].bitcast(I32))
         wv_raw = late[:, SLICES : SLICES + 4, :].rearrange("p (a x) m -> p a (x m)", a=2)
-        for k in range(SLICES // 2):
+        for k in range(EARLY_PAIRS):
             nc.sync.dma_start(
                 late[:, 2 * k : 2 * k + 2, :], ifm[256 * k : 256 * (k + 1), :].rearrange("(s p) m -> p s m", s=2)
             )
@@ -132,15 +132,21 @@ def tile_list_beam_slot_gating_kernel(
         w8_w = keep.tile([P, PASSES, N], U32, name="w8_w", tag="vw00", align_bytes=64)
         nc.sync.dma_start(w8_w[:].bitcast(I32), w8_words.rearrange("a p n i -> p a (n i)").bitcast(I32))
 
+        ifm_last = []
+        for i, tag in enumerate(("big0", "vw01")):
+            t = keep.tile([P, M], F32, name=f"ifm_last{i}", tag=tag, align_bytes=64)
+            nc.sync.dma_start(t[:], ifm[(SLICES - 2 + i) * P : (SLICES - 1 + i) * P, :])
+            ifm_last.append(t)
         for q in range(4):
             nc.sync.dma_start(
                 w4_s[32 * q + 4 : 32 * q + 8, :, 0:N].bitcast(I32),
                 w8_scales[:, 4 * q : 4 * q + 4, :].rearrange("a r n -> r a n").bitcast(I32),
             )
 
-        q_in = keep.tile([P, 4 * M], F32, name="q_in", tag="q_in", align_bytes=64)
-        z0_in = q_in[:, 0 : 2 * M]
-        wv_flat = q_in[:, 2 * M : 4 * M].bitcast(BF16)
+        z0_tile = keep.tile([P, 2 * M], F32, name="z0_in", tag="z0_in", align_bytes=64)
+        z0_in = z0_tile[:]
+        wv_tile = keep.tile([P, 4 * M], BF16, name="wv_bf", tag="wv_bf", align_bytes=64)
+        wv_flat = wv_tile[:]
         wv_bf = wv_flat.rearrange("p (a n j) -> p a n j", a=2, j=4)
         for a in range(PASSES):
             nc.scalar.copy(wv_bf[:, a, :, :], wv_raw[:, a, :].rearrange("p (j n) -> p n j", j=4))
@@ -156,18 +162,27 @@ def tile_list_beam_slot_gating_kernel(
 
         zt = {}
 
-        def turn_and_add(k, c, x_of):
+        zt_banks = {}
+
+        def turn_ifm(k, c):
+            bank = psum.tile([P, 2, 2, P], F32, name=f"A{k}{c}", tag=f"bank{4 * (k % 2) + c}")
+            zt_banks[(k, c)] = bank
+            for b in range(2):
+                for i in range(2):
+                    m0 = c * CHUNK + b * P
+                    nc.tensor.matmul(
+                        bank[:, b, i, :], late[:, 2 * k + i, m0 : m0 + P] if k < EARLY_PAIRS else ifm_last[i][:, m0 : m0 + P], ident[:],
+                        start=(b == 0 and i == 0), stop=False, is_transpose=True,
+                    )
+
+        def turn_x(k, c, x_of):
             g, j = divmod(k, 2)
-            bank = psum.tile([P, 2, 2, P], F32, name="zt_bank", tag=f"bank{4 + c}")
-            steps = [(True, b, i) for b in range(2) for i in range(2)] + [
-                (False, b, i) for b in range(2) for i in range(2)
-            ]
-            for n, (is_ifm, b, i) in enumerate(steps):
-                m0 = c * CHUNK + b * P
-                src = late[:, 2 * k + i, m0 : m0 + P] if is_ifm else x_of(i, b)
-                nc.tensor.matmul(
-                    bank[:, b, i, :], src, ident[:], start=(n == 0), stop=(n == len(steps) - 1), is_transpose=True
-                )
+            bank = zt_banks[(k, c)]
+            for i in range(2):
+                for b in range(2):
+                    nc.tensor.matmul(
+                        bank[:, b, i, :], x_of(i, b), ident[:], start=False, stop=(b == 1 and i == 1), is_transpose=True
+                    )
             if j == 0:
                 zt[(g, c)] = ring.tile([P, 2, 2, P, 2], BF16, name="zt", tag="zt", bufs=8, align_bytes=64)
             nc.scalar.copy(
@@ -176,7 +191,7 @@ def tile_list_beam_slot_gating_kernel(
             )
 
         def turn_back(g, c, dst):
-            bank = psum.tile([P, 2, 2, P], F32, name="z_bank", tag=f"bank{4 + c}")
+            bank = psum.tile([P, 2, 2, P], F32, name=f"B{g}{c}", tag=f"bank{4 + c}")
             words = zt[(g, c)][:].rearrange("m b u p e -> m (b u p e)").bitcast(F32)
             for b in range(2):
                 for u in range(2):
@@ -186,7 +201,9 @@ def tile_list_beam_slot_gating_kernel(
 
         z0_s = keep.tile([P, M], U8, name="z0_s", align_bytes=64)
 
-        for k in range(SLICES // 2):
+        for k in range(EARLY_PAIRS):
+            for c in range(CHUNKS):
+                turn_ifm(k, c)
             if k == 0:
                 for jh in range(2):
                     for s in range(2):
@@ -201,49 +218,54 @@ def tile_list_beam_slot_gating_kernel(
                     nc.vector.tensor_copy(x[:], page_of(2 * k + i)[:].indirect(list3[:]))
                     xs.append(x)
                 for c in range(CHUNKS):
-                    turn_and_add(k, c, lambda i, b: xs[i][:, c * CHUNK + b * P : c * CHUNK + (b + 1) * P])
+                    turn_x(k, c, lambda i, b: xs[i][:, c * CHUNK + b * P : c * CHUNK + (b + 1) * P])
                     if k == 1:
                         turn_back(0, c, z0_in[:, 2 * c * CHUNK : 2 * (c + 1) * CHUNK])
 
-        wv_w = keep.tile([P, PASSES, N], U32, name="wv_w", tag="h6", align_bytes=64)
-        z0_w = keep.tile([P, M], U32, name="z0_w", tag="h7", align_bytes=64)
-        xc = []
+        for c in range(CHUNKS):
+            turn_ifm(EARLY_PAIRS, c)
+        xc = {}
+        codes = {}
 
-        def late_gathers(c, tile):
+        def late_gathers(c, tag):
+            tile = keep.tile([P, 2, CHUNK], F32, name=f"xc{c}", tag=tag, align_bytes=64)
             for i in range(2):
                 nc.vector.tensor_copy(tile[:, i, :], pages[i][:].indirect(list3[:, 16 * c : 16 * (c + 1)]))
-            xc.append(tile)
+            xc[c] = tile
 
-        xc_first = keep.tile([P, 2, 2, CHUNK], F32, name="xc_first", align_bytes=64)
-        for c in range(2):
-            late_gathers(c, xc_first[:, c, :, :])
-        nc.vector.quantize_mx(out=z0_w[:].bitcast(FP8X4), scales=z0_s[:], in_=z0_in.bitcast(BF16))
-        nc.vector.quantize_mx(
-            out=wv_w[:].rearrange("p a n -> p (a n)").bitcast(FP8X4),
-            scales=wv_s[:].rearrange("p a n -> p (a n)"),
-            in_=wv_flat,
-        )
-        z1 = []
+        def quantise_z0(tag):
+            codes["z0"] = keep.tile([P, M], U32, name="z0_w", tag=tag, align_bytes=64)
+            nc.vector.quantize_mx(out=codes["z0"][:].bitcast(FP8X4), scales=z0_s[:], in_=z0_in.bitcast(BF16))
+
+        def quantise_wv(tag):
+            codes["wv"] = keep.tile([P, PASSES, N], U32, name="wv_w", tag=tag, align_bytes=64)
+            nc.vector.quantize_mx(
+                out=codes["wv"][:].rearrange("p a n -> p (a n)").bitcast(FP8X4),
+                scales=wv_s[:].rearrange("p a n -> p (a n)"),
+                in_=wv_flat,
+            )
+
+        z1 = {}
 
         def finish_z(c):
-            turn_and_add(EARLY_PAIRS, c, lambda i, b: xc[c][:, i, b * P : (b + 1) * P])
+            turn_x(EARLY_PAIRS, c, lambda i, b: xc[c][:, i, b * P : (b + 1) * P])
             z1_in = keep.tile([P, 2 * CHUNK], F32, name=f"z1_in{c}", tag=f"z1_in{c}", align_bytes=64)
             turn_back(1, c, z1_in[:])
             z1_w = ring.tile([P, CHUNK], U32, name="z1_w", tag="z1_w", bufs=4, align_bytes=64)
             z1_s = ring.tile([P, CHUNK], U8, name="z1_s", tag="z1_s", bufs=4, align_bytes=64)
             nc.vector.quantize_mx(out=z1_w[:].bitcast(FP8X4), scales=z1_s[:], in_=z1_in[:].bitcast(BF16))
-            z1.append((z1_w, z1_s))
+            z1[c] = (z1_w, z1_s)
 
         y_banks = {}
 
         def second_pass(c, q, w, a):
             cols = slice(c * CHUNK, (c + 1) * CHUNK)
             if a == 0:
-                y_banks[(c, q, w)] = psum.tile([P, 2, CHUNK], F32, name="y_bank", tag=f"bank{4 * (c % 2) + 2 * q + w}")
-                z_w, z_s = z0_w[:, cols], z0_s[:, cols]
+                y_banks[(c, q, w)] = psum.tile([P, 2, CHUNK], F32, name=f"Y{c}{q}{w}", tag=f"bank{2 * ((2 * c + q) % 3) + w}")
+                z_w, z_s = codes["z0"][:, cols], z0_s[:, cols]
             else:
                 z_w, z_s = z1[c][0][:], z1[c][1][:]
-            w_w, w_s, row = ((w8_w, w4_s, 4), (wv_w, wv_s, 0))[w]
+            w_w, w_s, row = ((w8_w, w4_s, 4), (codes.get("wv"), wv_s, 0))[w]
             for i in range(2):
                 n0 = (2 * q + i) * P
                 nc.tensor.matmul_mx(
@@ -265,21 +287,34 @@ def tile_list_beam_slot_gating_kernel(
             nc.vector.tensor_tensor(res[:], resp[:], gate[:], MULT)
             nc.sync.dma_start(out[256 * q : 256 * (q + 1), cols].rearrange("(i p) m -> p i m", i=2), res[:])
 
-        xc_rest = keep.tile([P, 2, 2, CHUNK], F32, name="xc_rest", tag="q_in", align_bytes=64)
-        for c in range(2, CHUNKS):
-            late_gathers(c, xc_rest[:, c - 2, :, :])
+        def unit(c, q):
+            for w in range(2):
+                if (c, q, w) not in y_banks:
+                    second_pass(c, q, w, 0)
+                second_pass(c, q, w, 1)
+            gate_and_store(c, q)
+
+        scatter(6,0,S)
+        scatter(7,0,S)
+        quantise_z0("h7")
+        second_pass(0,0,0,0)
+        second_pass(0,1,0,0)
+        late_gathers(0,"big0")
+        late_gathers(1,"vw01")
+        quantise_wv("big0")
+        late_gathers(2,"wv_bf")
         finish_z(0)
+        second_pass(0,0,1,0)
+        second_pass(0,1,1,0)
+        late_gathers(3,"z1_in0")
         finish_z(1)
-        for w in range(2):
-            for q in range(2):
-                second_pass(0, q, w, 0)
-        for c in range(CHUNKS):
-            if c == 1:
-                finish_z(2)
-                finish_z(3)
-            for q in range(2):
-                for w in range(2):
-                    if c > 0:
-                        second_pass(c, q, w, 0)
-                    second_pass(c, q, w, 1)
-                gate_and_store(c, q)
+        unit(0,0)
+        unit(0,1)
+        finish_z(2)
+        unit(1,0)
+        finish_z(3)
+        unit(1,1)
+        unit(2,0)
+        unit(2,1)
+        unit(3,0)
+        unit(3,1)

@@ -15,6 +15,7 @@ U8 = mybir.dt.uint8
 FP8X4 = mybir.dt.float8_e4m3fn_x4
 FP4X4 = mybir.dt.float4_e2m1fn_x4
 MULT = mybir.AluOpType.mult
+ADD = mybir.AluOpType.add
 SIGMOID = mybir.ActivationFunctionType.Sigmoid
 
 P = 128
@@ -167,22 +168,13 @@ def tile_list_beam_slot_gating_kernel(
         def turn_ifm(k, c):
             bank = psum.tile([P, 2, 2, P], F32, name=f"A{k}{c}", tag=f"bank{4 * (k % 2) + c}")
             zt_banks[(k, c)] = bank
-            for b in range(2):
-                for i in range(2):
-                    m0 = c * CHUNK + b * P
-                    nc.tensor.matmul(
-                        bank[:, b, i, :], late[:, 2 * k + i, m0 : m0 + P] if k < EARLY_PAIRS else ifm_last[i][:, m0 : m0 + P], ident[:],
-                        start=(b == 0 and i == 0), stop=False, is_transpose=True,
-                    )
 
         def turn_x(k, c, x_of):
             g, j = divmod(k, 2)
             bank = zt_banks[(k, c)]
             for i in range(2):
                 for b in range(2):
-                    nc.tensor.matmul(
-                        bank[:, b, i, :], x_of(i, b), ident[:], start=False, stop=(b == 1 and i == 1), is_transpose=True
-                    )
+                    nc.tensor.transpose(bank[:, b, i, :], x_of(i, b), ident[:])
             if j == 0:
                 zt[(g, c)] = ring.tile([P, 2, 2, P, 2], BF16, name="zt", tag="zt", bufs=8, align_bytes=64)
             nc.scalar.copy(
@@ -215,7 +207,7 @@ def tile_list_beam_slot_gating_kernel(
                 xs = []
                 for i in range(2):
                     x = ring.tile([P, M], F32, name="x", tag="x", bufs=6)
-                    nc.vector.tensor_copy(x[:], page_of(2 * k + i)[:].indirect(list3[:]))
+                    nc.vector.tensor_tensor(x[:], page_of(2 * k + i)[:].indirect(list3[:]), late[:, 2 * k + i, :], ADD)
                     xs.append(x)
                 for c in range(CHUNKS):
                     turn_x(k, c, lambda i, b: xs[i][:, c * CHUNK + b * P : c * CHUNK + (b + 1) * P])
@@ -230,7 +222,10 @@ def tile_list_beam_slot_gating_kernel(
         def late_gathers(c, tag):
             tile = keep.tile([P, 2, CHUNK], F32, name=f"xc{c}", tag=tag, align_bytes=64)
             for i in range(2):
-                nc.vector.tensor_copy(tile[:, i, :], pages[i][:].indirect(list3[:, 16 * c : 16 * (c + 1)]))
+                nc.vector.tensor_tensor(
+                    tile[:, i, :], pages[i][:].indirect(list3[:, 16 * c : 16 * (c + 1)]),
+                    ifm_last[i][:, c * CHUNK : (c + 1) * CHUNK], ADD,
+                )
             xc[c] = tile
 
         def quantise_z0(tag):
@@ -299,9 +294,9 @@ def tile_list_beam_slot_gating_kernel(
         quantise_z0("h7")
         second_pass(0,0,0,0)
         second_pass(0,1,0,0)
-        late_gathers(0,"big0")
-        late_gathers(1,"vw01")
-        quantise_wv("big0")
+        late_gathers(0,"xc0")
+        late_gathers(1,"xc1")
+        quantise_wv("h6")
         late_gathers(2,"wv_bf")
         finish_z(0)
         second_pass(0,0,1,0)

@@ -20,12 +20,11 @@ SIGMOID = mybir.ActivationFunctionType.Sigmoid
 
 P = 128
 PASSES = 2
-SLICES = H // P
 HALF = 512
 CHUNK = 256
 CHUNKS = M // CHUNK
-EARLY_PAIRS = 3
 FIRST = 2
+LAST_CUT = 768
 
 
 def tile_list_beam_slot_gating_kernel(
@@ -34,8 +33,13 @@ def tile_list_beam_slot_gating_kernel(
     nc = tc.nc
     with ExitStack() as ctx:
         keep = ctx.enter_context(tc.tile_pool(name="keep", bufs=1))
-        ring = ctx.enter_context(tc.tile_pool(name="ring", bufs=2))
         psum = ctx.enter_context(tc.psum_pool(name="psum", bufs=1))
+
+        def sb(shape, dtype, name, tag=None):
+            return keep.tile(shape, dtype, name=name, tag=tag or name, align_bytes=64)
+
+        def bank_tile(shape, name, index):
+            return psum.tile(shape, F32, name=name, tag=f"bank{index}")
 
         list1 = keep.tile([P, S // 16], U16, name="list1")
         list2 = keep.tile([P, S // 16], U16, name="list2")
@@ -44,7 +48,7 @@ def tile_list_beam_slot_gating_kernel(
         nc.sync.dma_start(list2[:], offs2)
         nc.sync.dma_start(list3[:], offs3)
 
-        tab_s = keep.tile([P, T], U8, name="tab_s", tag="late", align_bytes=64)
+        tab_s = sb([P, T], U8, "tab_s", "late")
         nc.gpsimd.memset(tab_s[:].bitcast(I32), 0)
         for q in range(4):
             nc.sync.dma_start(
@@ -52,63 +56,69 @@ def tile_list_beam_slot_gating_kernel(
             )
         tab_w = []
         for a in range(PASSES):
-            t = keep.tile([P, T], U32, name=f"tab_w{a}", tag=f"big{a}", align_bytes=64)
+            t = sb([P, T], U32, f"tab_w{a}", f"big{a}")
             nc.sync.dma_start(t[:].bitcast(I32), tab_words[a].rearrange("p t i -> p (t i)").bitcast(I32))
             tab_w.append(t)
 
         w4_hbm = w4_words.rearrange("a p n -> p a n")
-        w4_first = keep.tile([P, PASSES, 2 * P * FIRST], U8, name="w4_first", align_bytes=64)
+        w4_first = sb([P, PASSES, 2 * P * FIRST], U8, "w4_first")
         nc.sync.dma_start(w4_first[:].bitcast(I32), w4_hbm[:, :, 0 : 2 * P * FIRST].bitcast(I32))
-        w4_s = keep.tile([P, PASSES, H], U8, name="w4_s", align_bytes=64)
+        w4_s = sb([P, PASSES, H], U8, "w4_s")
         nc.vector.memset(w4_s[:].rearrange("p a n -> p (a n)").bitcast(I32), 0)
         for q in range(4):
             nc.sync.dma_start(
                 w4_s[32 * q : 32 * q + 4, :, :].bitcast(I32),
                 w4_scales[:, 4 * q : 4 * q + 4, :].rearrange("a r n -> r a n").bitcast(I32),
             )
-        v_s1 = keep.tile([P, S], U8, name="v_s1", align_bytes=64)
+        v_s1 = sb([P, S], U8, "v_s1")
         nc.vector.memset(v_s1[:].bitcast(I32), 0)
 
-        page0 = keep.tile([P, T2], F32, name="page0", align_bytes=64)
-        nc.vector.memset(page0[:].bitcast(I32), 0)
-
-        v_s0 = keep.tile([P, S], U8, name="v_s0", align_bytes=64)
-        nc.vector.tensor_copy(v_s0[:], tab_s[:].indirect(list1[:]))
-        nc.scalar.dma_start(v_s1[0:112, :].bitcast(I32), v_s0[4:116, :].bitcast(I32))
-        v_s = [v_s0, v_s1]
-
-
-        v_w = {}
-        for a, jh in ((0, 0), (0, 1), (1, 0), (1, 1)):
-            t = keep.tile([P, HALF], U32, name=f"v_w{a}{jh}", tag=f"vw{a}{jh}", align_bytes=64)
-            nc.vector.tensor_copy(t[:], tab_w[a][:].indirect(list1[:, 32 * jh : 32 * jh + 32]))
-            v_w[(a, jh)] = t
-
-        page1 = keep.tile([P, T2], F32, name="page1", tag="big1", align_bytes=64)
-        nc.vector.memset(page1[:].bitcast(I32), 0)
-        pages = [page0, page1]
+        pages = [sb([P, T2], F32, f"page{i}") for i in range(2)]
+        nc.vector.memset(pages[0][:].bitcast(I32), 0)
+        nc.gpsimd.memset(pages[1][:].bitcast(I32), 0)
 
         ident = keep.tile([P, P], F32, name="ident")
         make_identity(nc, ident[:])
 
-        late = keep.tile([P, SLICES + 5, M], F32, name="late", tag="late", align_bytes=64)
-        wgs_sb = late[:, SLICES + 4, :]
+        v_s0 = sb([P, S], U8, "v_s0")
+        nc.vector.tensor_copy(v_s0[:], tab_s[:].indirect(list1[:]))
+        nc.scalar.dma_start(v_s1[0:112, :].bitcast(I32), v_s0[4:116, :].bitcast(I32))
+        v_s = [v_s0, v_s1]
+
+        v_w = {}
+        for a in range(PASSES):
+            for jh in range(2):
+                t = sb([P, HALF], U32, f"v_w{a}{jh}")
+                nc.vector.tensor_copy(t[:], tab_w[a][:].indirect(list1[:, 32 * jh : 32 * jh + 32]))
+                v_w[(a, jh)] = t
+
+        late = sb([P, 17, M], F32, "late")
+        wgs_sb = late[:, 0, :]
+        ifm_nat = late[:, 1:5, :]
+        ifm_dealt = late[:, 5:9, :]
+        wgs_dealt = late[:, 9:13, :]
+        wv_raw = late[:, 13:17, :].rearrange("p (a x) m -> p a (x m)", a=2)
         for jh in range(2):
             nc.sync.dma_start(wgs_sb[:, jh * HALF : (jh + 1) * HALF], wgs[:, jh * HALF : (jh + 1) * HALF])
-        w4_rest = keep.tile([P, PASSES, 2 * (H - P * FIRST)], U8, name="w4_rest", tag="big0", align_bytes=64)
-        nc.sync.dma_start(w4_rest[:].bitcast(I32), w4_hbm[:, :, 2 * P * FIRST : 2 * H].bitcast(I32))
-        wv_raw = late[:, SLICES : SLICES + 4, :].rearrange("p (a x) m -> p a (x m)", a=2)
-        for k in range(EARLY_PAIRS):
+        w4_rest = sb([P, PASSES, 2 * (H - P * FIRST)], U8, "w4_rest")
+        w4_gate = w4_rest[:].bitcast(I32)
+        nc.sync.dma_start(w4_gate, w4_hbm[:, :, 2 * P * FIRST : 2 * H].bitcast(I32))
+        for k in range(2):
             nc.sync.dma_start(
-                late[:, 2 * k : 2 * k + 2, :], ifm[256 * k : 256 * (k + 1), :].rearrange("(s p) m -> p s m", s=2)
+                ifm_nat[:, 2 * k : 2 * k + 2, :], ifm[256 * k : 256 * (k + 1), :].rearrange("(s p) m -> p s m", s=2)
             )
-            if k == 1:
+            if k == 0:
                 nc.sync.dma_start(wv_raw, wv.rearrange("(a p j) n -> p a (j n)", a=2, j=4))
+        for g in range(4):
+            nc.sync.dma_start(wgs_dealt[32 * g : 32 * (g + 1), :, :], wgs.rearrange("(q t) j -> q t j", t=4))
+        ifm_hi = ifm[HALF:H, :].rearrange("(p t) m -> p t m", t=4)
+        for u in range(2):
+            nc.sync.dma_start(ifm_dealt[:, 2 * u : 2 * u + 2, :], ifm_hi[:, 2 * u : 2 * u + 2, :])
 
-        h = [keep.tile([P, S], F32, name=f"h{s}", tag=f"h{s}", align_bytes=64) for s in range(SLICES)]
+        h = [sb([P, S], F32, f"h{s}") for s in range(4)]
 
         def first_product(s, jh):
-            bank = psum.tile([P, HALF], F32, name="h_bank", tag=f"bank{2 * jh + s % 2}")
+            bank = bank_tile([P, HALF], f"h_bank{s}{jh}", 2 * jh + s % 2)
             w4 = w4_first if s < FIRST else w4_rest
             c0 = 2 * P * (s if s < FIRST else s - FIRST)
             for a in range(PASSES):
@@ -126,141 +136,153 @@ def tile_list_beam_slot_gating_kernel(
         for jh in range(2):
             for s in range(FIRST):
                 first_product(s, jh)
-        for s in range(FIRST, SLICES):
+        for s in range(FIRST, 4):
             for jh in range(2):
                 first_product(s, jh)
 
-        w8_w = keep.tile([P, PASSES, N], U32, name="w8_w", tag="vw00", align_bytes=64)
-        nc.sync.dma_start(w8_w[:].bitcast(I32), w8_words.rearrange("a p n i -> p a (n i)").bitcast(I32))
+        h_t = [sb([P, 4, 4, P], F32, f"h_t{jh}", f"big{jh}") for jh in range(2)]
+        c_hi = 2 * (HALF - P * FIRST)
+        for jh in range(2):
+            for i in range(4):
+                bank = bank_tile([P, HALF], f"ht_bank{jh}{i}", 4 + i)
+                j0 = jh * HALF + i * P
+                for a in range(PASSES):
+                    nc.tensor.matmul_mx(
+                        out=bank[:],
+                        lhsT=v_w[(a, jh)][:, i * P : (i + 1) * P].bitcast(FP8X4),
+                        lhsT_scale=v_s[a][:, j0 : j0 + P],
+                        rhs=w4_rest[:, a, c_hi : c_hi + 2 * HALF].bitcast(FP4X4),
+                        rhs_scale=w4_s[:, a, HALF:H],
+                        start=(a == 0),
+                        stop=(a == PASSES - 1),
+                    )
+                nc.scalar.copy(h_t[jh][:, i, :, :], bank[:].rearrange("j (q t) -> j t q", t=4))
 
-        ifm_last = []
-        for i, tag in enumerate(("big0", "vw01")):
-            t = keep.tile([P, M], F32, name=f"ifm_last{i}", tag=tag, align_bytes=64)
-            nc.sync.dma_start(t[:], ifm[(SLICES - 2 + i) * P : (SLICES - 1 + i) * P, :])
-            ifm_last.append(t)
+        wv_tile = sb([P, 4 * M], BF16, "wv_bf")
+        wv_bf = wv_tile[:].rearrange("p (a n j) -> p a n j", a=2, j=4)
+        for a in range(PASSES):
+            nc.scalar.copy(wv_bf[:, a, :, :], wv_raw[:, a, :].rearrange("p (j n) -> p n j", j=4))
+
+        def turn_plane(t, jh, pieces):
+            bank = bank_tile([P, 4, P], f"plane_bank{t}{jh}", 2 * jh + t % 2)
+            for i in range(4):
+                nc.tensor.transpose(bank[:, i, :], h_t[jh][:, i, t, :], ident[:])
+            flat = bank[:].rearrange("p i j -> p (i j)")
+            for dst, lo, hi in pieces:
+                nc.scalar.copy(dst, flat[:, lo:hi])
+
+        w8_w = sb([P, PASSES, N], U32, "w8_w", "v_w00")
+        nc.sync.dma_start(w8_w[:].bitcast(I32), w8_words.rearrange("a p n i -> p a (n i)").bitcast(I32))
         for q in range(4):
             nc.sync.dma_start(
                 w4_s[32 * q + 4 : 32 * q + 8, :, 0:N].bitcast(I32),
                 w8_scales[:, 4 * q : 4 * q + 4, :].rearrange("a r n -> r a n").bitcast(I32),
             )
 
-        z0_tile = keep.tile([P, 2 * M], F32, name="z0_in", tag="z0_in", align_bytes=64)
-        z0_in = z0_tile[:]
-        wv_tile = keep.tile([P, 4 * M], BF16, name="wv_bf", tag="wv_bf", align_bytes=64)
-        wv_flat = wv_tile[:]
-        wv_bf = wv_flat.rearrange("p (a n j) -> p a n j", a=2, j=4)
-        for a in range(PASSES):
-            nc.scalar.copy(wv_bf[:, a, :, :], wv_raw[:, a, :].rearrange("p (j n) -> p n j", j=4))
-        wv_s = keep.tile([P, PASSES, N], U8, name="wv_s", align_bytes=64)
+        def scatter(page, values, weights, lo, hi):
+            nc.vector.tensor_tensor(page[:].indirect(list2[:, lo // 16 : hi // 16]), values, weights, MULT)
 
-        def page_of(s):
-            return pages[s % 2]
+        def gather(dst, page, extra, lo, hi):
+            nc.vector.tensor_tensor(dst, page[:].indirect(list3[:, lo // 16 : hi // 16]), extra, ADD)
 
-        def scatter(s, lo, hi):
-            nc.vector.tensor_tensor(
-                page_of(s)[:].indirect(list2[:, lo // 16 : hi // 16]), h[s][:, lo:hi], wgs_sb[:, lo:hi], MULT
-            )
-
-        zt = {}
-
-        zt_banks = {}
-
-        def turn_ifm(k, c):
-            bank = psum.tile([P, 2, 2, P], F32, name=f"A{k}{c}", tag=f"bank{4 * (k % 2) + c}")
-            zt_banks[(k, c)] = bank
-
-        def turn_x(k, c, x_of):
-            g, j = divmod(k, 2)
-            bank = zt_banks[(k, c)]
+        zt = [sb([P, 2, 2, P, 2], BF16, f"zt{c}") for c in range(CHUNKS)]
+        z0_in = sb([P, 2 * M], F32, "z0_in")
+        hp = {}
+        for k in range(2):
+            if k == 0:
+                for jh in range(2):
+                    for i in range(2):
+                        cols = slice(jh * HALF, (jh + 1) * HALF)
+                        scatter(pages[i], h[i][:, cols], wgs_sb[:, cols], jh * HALF, (jh + 1) * HALF)
+            else:
+                for i in range(2):
+                    scatter(pages[i], h[2 + i][:], wgs_sb, 0, S)
+            x = sb([P, 2, M], F32, f"x{k}")
             for i in range(2):
-                for b in range(2):
-                    nc.tensor.transpose(bank[:, b, i, :], x_of(i, b), ident[:])
-            if j == 0:
-                zt[(g, c)] = ring.tile([P, 2, 2, P, 2], BF16, name="zt", tag="zt", bufs=8, align_bytes=64)
-            nc.scalar.copy(
-                zt[(g, c)][:, :, :, 64 * j : 64 * (j + 1), :],
-                bank[:].rearrange("m b i r -> m b (i r)").rearrange("m b (p u e) -> m b u p e", u=2, e=2),
-            )
-
-        def turn_back(g, c, dst):
-            bank = psum.tile([P, 2, 2, P], F32, name=f"B{g}{c}", tag=f"bank{4 + c}")
-            words = zt[(g, c)][:].rearrange("m b u p e -> m (b u p e)").bitcast(F32)
+                gather(x[:, i, :], pages[i], ifm_nat[:, 2 * k + i, :], 0, M)
+            if k == 0:
+                for t in range(2):
+                    hp[t] = sb([P, S], F32, f"hp{t}", f"h{t}")
+                    for jh in range(2):
+                        turn_plane(t, jh, [(hp[t][:, jh * HALF : (jh + 1) * HALF], 0, HALF)])
+            for c in range(CHUNKS):
+                bank = bank_tile([P, 2, 2, P], f"A{k}{c}", 4 + c)
+                for i in range(2):
+                    for b in range(2):
+                        m0 = c * CHUNK + b * P
+                        nc.tensor.transpose(bank[:, b, i, :], x[:, i, m0 : m0 + P], ident[:])
+                nc.scalar.copy(
+                    zt[c][:, :, :, 64 * k : 64 * (k + 1), :],
+                    bank[:].rearrange("m b i r -> m b (i r)").rearrange("m b (p u e) -> m b u p e", u=2, e=2),
+                )
+        for c in range(CHUNKS):
+            bank = bank_tile([P, 2, 2, P], f"B{c}", c)
+            words = zt[c][:].rearrange("m b u p e -> m (b u p e)").bitcast(F32)
             for b in range(2):
                 for u in range(2):
                     w0 = (2 * b + u) * P
                     nc.tensor.transpose(bank[:, b, u, :], words[:, w0 : w0 + P], ident[:])
+            dst = z0_in[:, 2 * c * CHUNK : 2 * (c + 1) * CHUNK]
             nc.scalar.copy(dst.rearrange("p (b m u) -> p b m u", b=2, u=2), bank[:].rearrange("p b u m -> p b m u"))
 
-        z0_s = keep.tile([P, M], U8, name="z0_s", align_bytes=64)
+        wv_s = sb([P, PASSES, N], U8, "wv_s")
+        wv_w = sb([P, PASSES, N], U32, "wv_w")
+        nc.vector.quantize_mx(
+            out=wv_w[:].rearrange("p a n -> p (a n)").bitcast(FP8X4),
+            scales=wv_s[:].rearrange("p a n -> p (a n)"),
+            in_=wv_tile[:],
+        )
 
-        for k in range(EARLY_PAIRS):
-            for c in range(CHUNKS):
-                turn_ifm(k, c)
-            if k == 0:
-                for jh in range(2):
-                    for s in range(2):
-                        scatter(s, jh * HALF, (jh + 1) * HALF)
-            else:
-                scatter(2 * k, 0, S)
-                scatter(2 * k + 1, 0, S)
-            if k < EARLY_PAIRS:
-                xs = []
-                for i in range(2):
-                    x = ring.tile([P, M], F32, name="x", tag="x", bufs=6)
-                    nc.vector.tensor_tensor(x[:], page_of(2 * k + i)[:].indirect(list3[:]), late[:, 2 * k + i, :], ADD)
-                    xs.append(x)
-                for c in range(CHUNKS):
-                    turn_x(k, c, lambda i, b: xs[i][:, c * CHUNK + b * P : c * CHUNK + (b + 1) * P])
-                    if k == 1:
-                        turn_back(0, c, z0_in[:, 2 * c * CHUNK : 2 * (c + 1) * CHUNK])
-
+        for t in range(2):
+            scatter(pages[t], hp[t][:], wgs_dealt[:, t, :], 0, S)
+        x01 = sb([P, 2, M], F32, "x01", "x0")
+        for t in range(2):
+            gather(x01[:, t, :], pages[t], ifm_dealt[:, t, :], 0, M)
+        z1_in = [sb([P, CHUNK, 4], BF16, f"z1_in{c}", f"zt{c}") for c in range(CHUNKS)]
         for c in range(CHUNKS):
-            turn_ifm(EARLY_PAIRS, c)
-        xc = {}
-        codes = {}
+            cols = slice(c * CHUNK, (c + 1) * CHUNK)
+            nc.scalar.copy(z1_in[c][:, :, 0:2], x01[:, :, cols].rearrange("p e m -> p m e"))
 
-        def late_gathers(c, tag):
-            tile = keep.tile([P, 2, CHUNK], F32, name=f"xc{c}", tag=tag, align_bytes=64)
-            for i in range(2):
-                nc.vector.tensor_tensor(
-                    tile[:, i, :], pages[i][:].indirect(list3[:, 16 * c : 16 * (c + 1)]),
-                    ifm_last[i][:, c * CHUNK : (c + 1) * CHUNK], ADD,
-                )
-            xc[c] = tile
-
-        def quantise_z0(tag):
-            codes["z0"] = keep.tile([P, M], U32, name="z0_w", tag=tag, align_bytes=64)
-            nc.vector.quantize_mx(out=codes["z0"][:].bitcast(FP8X4), scales=z0_s[:], in_=z0_in.bitcast(BF16))
-
-        def quantise_wv(tag):
-            codes["wv"] = keep.tile([P, PASSES, N], U32, name="wv_w", tag=tag, align_bytes=64)
-            nc.vector.quantize_mx(
-                out=codes["wv"][:].rearrange("p a n -> p (a n)").bitcast(FP8X4),
-                scales=wv_s[:].rearrange("p a n -> p (a n)"),
-                in_=wv_flat,
-            )
+        hp[2] = sb([P, S], F32, "hp2", "wv_bf")
+        for jh in range(2):
+            turn_plane(2, jh, [(hp[2][:, jh * HALF : (jh + 1) * HALF], 0, HALF)])
+        hp3a = sb([P, LAST_CUT], F32, "hp3a", "h2")
+        hp3b = sb([P, S - LAST_CUT], F32, "hp3b", "h3")
+        turn_plane(3, 0, [(hp3a[:, 0:HALF], 0, HALF)])
+        turn_plane(3, 1, [(hp3a[:, HALF:LAST_CUT], 0, LAST_CUT - HALF), (hp3b[:], LAST_CUT - HALF, HALF)])
+        scatter(pages[0], hp[2][:], wgs_dealt[:, 2, :], 0, S)
+        scatter(pages[1], hp3a[:], wgs_dealt[:, 3, 0:LAST_CUT], 0, LAST_CUT)
+        z0_w = sb([P, M], U32, "z0_w", "h2")
+        z0_s = sb([P, M], U8, "z0_s")
+        nc.vector.quantize_mx(out=z0_w[:].bitcast(FP8X4), scales=z0_s[:], in_=z0_in[:].bitcast(BF16))
+        scatter(pages[1], hp3b[:], wgs_dealt[:, 3, LAST_CUT:S], LAST_CUT, S)
 
         z1 = {}
-
-        def finish_z(c):
-            turn_x(EARLY_PAIRS, c, lambda i, b: xc[c][:, i, b * P : (b + 1) * P])
-            z1_in = keep.tile([P, 2 * CHUNK], F32, name=f"z1_in{c}", tag=f"z1_in{c}", align_bytes=64)
-            turn_back(1, c, z1_in[:])
-            z1_w = ring.tile([P, CHUNK], U32, name="z1_w", tag="z1_w", bufs=4, align_bytes=64)
-            z1_s = ring.tile([P, CHUNK], U8, name="z1_s", tag="z1_s", bufs=4, align_bytes=64)
-            nc.vector.quantize_mx(out=z1_w[:].bitcast(FP8X4), scales=z1_s[:], in_=z1_in[:].bitcast(BF16))
-            z1[c] = (z1_w, z1_s)
-
         y_banks = {}
+
+        def late_gathers(c):
+            cols = slice(c * CHUNK, (c + 1) * CHUNK)
+            xc = sb([P, 2, CHUNK], F32, f"xc{c}")
+            for i in range(2):
+                gather(xc[:, i, :], pages[i], ifm_dealt[:, 2 + i, cols], c * CHUNK, (c + 1) * CHUNK)
+            nc.scalar.copy(z1_in[c][:, :, 2:4], xc[:].rearrange("p e m -> p m e"))
+
+        def quantise_z1(c):
+            z1_w = sb([P, CHUNK], U32, f"z1_w{c}")
+            z1_s = sb([P, CHUNK], U8, f"z1_s{c}")
+            nc.vector.quantize_mx(
+                out=z1_w[:].bitcast(FP8X4), scales=z1_s[:], in_=z1_in[c][:].rearrange("p m t -> p (m t)")
+            )
+            z1[c] = (z1_w, z1_s)
 
         def second_pass(c, q, w, a):
             cols = slice(c * CHUNK, (c + 1) * CHUNK)
             if a == 0:
-                y_banks[(c, q, w)] = psum.tile([P, 2, CHUNK], F32, name=f"Y{c}{q}{w}", tag=f"bank{2 * ((2 * c + q) % 3) + w}")
-                z_w, z_s = codes["z0"][:, cols], z0_s[:, cols]
+                y_banks[(c, q, w)] = bank_tile([P, 2, CHUNK], f"Y{c}{q}{w}", 4 * (c % 2) + 2 * q + w)
+                z_w, z_s = z0_w[:, cols], z0_s[:, cols]
             else:
                 z_w, z_s = z1[c][0][:], z1[c][1][:]
-            w_w, w_s, row = ((w8_w, w4_s, 4), (codes.get("wv"), wv_s, 0))[w]
+            w_w, w_s, row = ((w8_w, w4_s, 4), (wv_w, wv_s, 0))[w]
             for i in range(2):
                 n0 = (2 * q + i) * P
                 nc.tensor.matmul_mx(
@@ -273,43 +295,30 @@ def tile_list_beam_slot_gating_kernel(
                     stop=(a == PASSES - 1 and i == 1),
                 )
 
-        def gate_and_store(c, q):
-            cols = slice(c * CHUNK, (c + 1) * CHUNK)
-            logit, resp = y_banks[(c, q, 0)], y_banks[(c, q, 1)]
-            gate = ring.tile([P, 2, CHUNK], F32, name="gate", tag="gate", bufs=4)
-            nc.scalar.activation(gate[:], logit[:], SIGMOID)
-            res = ring.tile([P, 2, CHUNK], F32, name="res", tag="res", bufs=4)
-            nc.vector.tensor_tensor(res[:], resp[:], gate[:], MULT)
-            nc.sync.dma_start(out[256 * q : 256 * (q + 1), cols].rearrange("(i p) m -> p i m", i=2), res[:])
-
         def unit(c, q):
             for w in range(2):
                 if (c, q, w) not in y_banks:
                     second_pass(c, q, w, 0)
                 second_pass(c, q, w, 1)
-            gate_and_store(c, q)
+            cols = slice(c * CHUNK, (c + 1) * CHUNK)
+            gate = sb([P, 2, CHUNK], F32, f"gate{c}{q}", f"gate{c % 2}{q}")
+            nc.scalar.activation(gate[:], y_banks[(c, q, 0)][:], SIGMOID)
+            res = sb([P, 2, CHUNK], F32, f"res{c}{q}", f"res{c % 2}{q}")
+            nc.vector.tensor_tensor(res[:], y_banks[(c, q, 1)][:], gate[:], MULT)
+            nc.sync.dma_start(out[256 * q : 256 * (q + 1), cols].rearrange("(i p) m -> p i m", i=2), res[:])
 
-        scatter(6,0,S)
-        scatter(7,0,S)
-        quantise_z0("h7")
-        second_pass(0,0,0,0)
-        second_pass(0,1,0,0)
-        late_gathers(0,"xc0")
-        late_gathers(1,"xc1")
-        quantise_wv("h6")
-        late_gathers(2,"wv_bf")
-        finish_z(0)
-        second_pass(0,0,1,0)
-        second_pass(0,1,1,0)
-        late_gathers(3,"z1_in0")
-        finish_z(1)
-        unit(0,0)
-        unit(0,1)
-        finish_z(2)
-        unit(1,0)
-        finish_z(3)
-        unit(1,1)
-        unit(2,0)
-        unit(2,1)
-        unit(3,0)
-        unit(3,1)
+        for c in range(2):
+            for q in range(2):
+                for w in range(2):
+                    second_pass(c, q, w, 0)
+        late_gathers(0)
+        for c in range(CHUNKS):
+            if c + 1 < CHUNKS:
+                late_gathers(c + 1)
+            quantise_z1(c)
+            if c >= 2:
+                for q in range(2):
+                    unit(c - 2, q)
+        for c in range(CHUNKS - 2, CHUNKS):
+            for q in range(2):
+                unit(c, q)

@@ -23,7 +23,7 @@ PASSES = 2
 HALF = 512
 CHUNK = 256
 CHUNKS = M // CHUNK
-FIRST = 2
+FIRST = 1
 LAST_CUT = 768
 
 
@@ -48,7 +48,7 @@ def tile_list_beam_slot_gating_kernel(
         nc.sync.dma_start(list2[:], offs2)
         nc.sync.dma_start(list3[:], offs3)
 
-        tab_s = sb([P, T], U8, "tab_s", "late")
+        tab_s = sb([P, T], U8, "tab_s")
         nc.gpsimd.memset(tab_s[:].bitcast(I32), 0)
         for q in range(4):
             nc.sync.dma_start(
@@ -70,12 +70,17 @@ def tile_list_beam_slot_gating_kernel(
                 w4_s[32 * q : 32 * q + 4, :, :].bitcast(I32),
                 w4_scales[:, 4 * q : 4 * q + 4, :].rearrange("a r n -> r a n").bitcast(I32),
             )
+        wgs_sb = sb([P, S], F32, "wgs_sb")
+        nc.sync.dma_start(wgs_sb[:], wgs)
         v_s1 = sb([P, S], U8, "v_s1")
         nc.vector.memset(v_s1[:].bitcast(I32), 0)
 
         pages = [sb([P, T2], F32, f"page{i}") for i in range(2)]
         nc.vector.memset(pages[0][:].bitcast(I32), 0)
         nc.gpsimd.memset(pages[1][:].bitcast(I32), 0)
+
+        warm = sb([P, 8], F32, "warm")
+        nc.scalar.activation(warm[:, 0:1], pages[0][:, 0:1], SIGMOID)
 
         ident = keep.tile([P, P], F32, name="ident")
         make_identity(nc, ident[:])
@@ -92,17 +97,13 @@ def tile_list_beam_slot_gating_kernel(
                 nc.vector.tensor_copy(t[:], tab_w[a][:].indirect(list1[:, 32 * jh : 32 * jh + 32]))
                 v_w[(a, jh)] = t
 
-        late = sb([P, 17, M], F32, "late")
-        wgs_sb = late[:, 0, :]
-        ifm_nat = late[:, 1:5, :]
-        ifm_dealt = late[:, 5:9, :]
-        wgs_dealt = late[:, 9:13, :]
-        wv_raw = late[:, 13:17, :].rearrange("p (a x) m -> p a (x m)", a=2)
-        for jh in range(2):
-            nc.sync.dma_start(wgs_sb[:, jh * HALF : (jh + 1) * HALF], wgs[:, jh * HALF : (jh + 1) * HALF])
-        w4_rest = sb([P, PASSES, 2 * (H - P * FIRST)], U8, "w4_rest")
-        w4_gate = w4_rest[:].bitcast(I32)
-        nc.sync.dma_start(w4_gate, w4_hbm[:, :, 2 * P * FIRST : 2 * H].bitcast(I32))
+        late = sb([P, 16, M], F32, "late", "big0")
+        ifm_nat = late[:, 0:4, :]
+        ifm_dealt = late[:, 4:8, :]
+        wgs_dealt = late[:, 8:12, :]
+        wv_raw = late[:, 12:16, :].rearrange("p (a x) m -> p a (x m)", a=2)
+        w4_rest = sb([P, PASSES, 2 * (H - P * FIRST)], U8, "w4_rest", "tab_s")
+        nc.sync.dma_start(w4_rest[:].bitcast(I32), w4_hbm[:, :, 2 * P * FIRST : 2 * H].bitcast(I32))
         for k in range(2):
             nc.sync.dma_start(
                 ifm_nat[:, 2 * k : 2 * k + 2, :], ifm[256 * k : 256 * (k + 1), :].rearrange("(s p) m -> p s m", s=2)
@@ -134,13 +135,13 @@ def tile_list_beam_slot_gating_kernel(
             nc.scalar.copy(h[s][:, jh * HALF : (jh + 1) * HALF], bank[:])
 
         for jh in range(2):
-            for s in range(FIRST):
+            for s in range(2):
                 first_product(s, jh)
-        for s in range(FIRST, 4):
+        for s in range(2, 4):
             for jh in range(2):
                 first_product(s, jh)
 
-        h_t = [sb([P, 4, 4, P], F32, f"h_t{jh}", f"big{jh}") for jh in range(2)]
+        h_t = [sb([P, 4, 4, P], F32, f"h_t{jh}", ("h_t0", "big1")[jh]) for jh in range(2)]
         c_hi = 2 * (HALF - P * FIRST)
         for jh in range(2):
             for i in range(4):
@@ -196,7 +197,7 @@ def tile_list_beam_slot_gating_kernel(
                         scatter(pages[i], h[i][:, cols], wgs_sb[:, cols], jh * HALF, (jh + 1) * HALF)
             else:
                 for i in range(2):
-                    scatter(pages[i], h[2 + i][:], wgs_sb, 0, S)
+                    scatter(pages[i], h[2 + i][:], wgs_sb[:], 0, S)
             x = sb([P, 2, M], F32, f"x{k}")
             for i in range(2):
                 gather(x[:, i, :], pages[i], ifm_nat[:, 2 * k + i, :], 0, M)
@@ -258,14 +259,18 @@ def tile_list_beam_slot_gating_kernel(
         scatter(pages[1], hp3b[:], wgs_dealt[:, 3, LAST_CUT:S], LAST_CUT, S)
 
         z1 = {}
+        xc = {}
+        gates = {}
         y_banks = {}
 
         def late_gathers(c):
             cols = slice(c * CHUNK, (c + 1) * CHUNK)
-            xc = sb([P, 2, CHUNK], F32, f"xc{c}")
+            xc[c] = sb([P, 2, CHUNK], F32, f"xc{c}", f"xc{c % 2}")
             for i in range(2):
-                gather(xc[:, i, :], pages[i], ifm_dealt[:, 2 + i, cols], c * CHUNK, (c + 1) * CHUNK)
-            nc.scalar.copy(z1_in[c][:, :, 2:4], xc[:].rearrange("p e m -> p m e"))
+                gather(xc[c][:, i, :], pages[i], ifm_dealt[:, 2 + i, cols], c * CHUNK, (c + 1) * CHUNK)
+
+        def weave(c):
+            nc.scalar.copy(z1_in[c][:, :, 2:4], xc[c][:].rearrange("p e m -> p m e"))
 
         def quantise_z1(c):
             z1_w = sb([P, CHUNK], U32, f"z1_w{c}")
@@ -295,14 +300,17 @@ def tile_list_beam_slot_gating_kernel(
                     stop=(a == PASSES - 1 and i == 1),
                 )
 
-        def unit(c, q):
+        def products(c, q):
             for w in range(2):
                 if (c, q, w) not in y_banks:
                     second_pass(c, q, w, 0)
                 second_pass(c, q, w, 1)
+            gates[(c, q)] = sb([P, 2, CHUNK], F32, f"gate{c}{q}", f"gate{c % 2}{q}")
+            nc.scalar.activation(gates[(c, q)][:], y_banks[(c, q, 0)][:], SIGMOID)
+
+        def finish(c, q):
             cols = slice(c * CHUNK, (c + 1) * CHUNK)
-            gate = sb([P, 2, CHUNK], F32, f"gate{c}{q}", f"gate{c % 2}{q}")
-            nc.scalar.activation(gate[:], y_banks[(c, q, 0)][:], SIGMOID)
+            gate = gates[(c, q)]
             res = sb([P, 2, CHUNK], F32, f"res{c}{q}", f"res{c % 2}{q}")
             nc.vector.tensor_tensor(res[:], y_banks[(c, q, 1)][:], gate[:], MULT)
             nc.sync.dma_start(out[256 * q : 256 * (q + 1), cols].rearrange("(i p) m -> p i m", i=2), res[:])
@@ -311,14 +319,20 @@ def tile_list_beam_slot_gating_kernel(
             for q in range(2):
                 for w in range(2):
                     second_pass(c, q, w, 0)
-        late_gathers(0)
+        for c in range(2):
+            late_gathers(c)
+            weave(c)
+        quantise_z1(0)
         for c in range(CHUNKS):
-            if c + 1 < CHUNKS:
-                late_gathers(c + 1)
-            quantise_z1(c)
-            if c >= 2:
-                for q in range(2):
-                    unit(c - 2, q)
-        for c in range(CHUNKS - 2, CHUNKS):
+            if c + 2 < CHUNKS:
+                late_gathers(c + 2)
             for q in range(2):
-                unit(c, q)
+                products(c, q)
+            if c + 2 < CHUNKS:
+                weave(c + 2)
+            if c >= 1:
+                finish(c - 1, 1)
+            if c + 1 < CHUNKS:
+                quantise_z1(c + 1)
+            finish(c, 0)
+        finish(CHUNKS - 1, 1)

@@ -45,50 +45,53 @@ def tile_list_beam_slot_gating_kernel(
         list2 = keep.tile([P, S // 16], U16, name="list2")
         list3 = keep.tile([P, M // 16], U16, name="list3")
         nc.sync.dma_start(list1[:], offs)
+
+        tab_s = sb([P, T], U8, "tab_s")
+        nc.sync.dma_start(tab_s[0:32, :].bitcast(I32), tab_scales.rearrange("a q t -> q a t").bitcast(I32))
+        nc.vector.memset(tab_s[32:64, :].bitcast(I32), 0)
+        nc.vector.memset(tab_s[64:P, :].bitcast(I32), 0)
         nc.sync.dma_start(list2[:], offs2)
         nc.sync.dma_start(list3[:], offs3)
 
-        tab_s = sb([P, T], U8, "tab_s")
-        nc.gpsimd.memset(tab_s[:].bitcast(I32), 0)
-        for q in range(4):
-            nc.sync.dma_start(
-                tab_s[32 * q : 32 * q + 8, :].bitcast(I32), tab_scales[:, 4 * q : 4 * q + 4, :].bitcast(I32)
-            )
+        w4_s = sb([P, PASSES, H], U8, "w4_s")
+        nc.gpsimd.memset(w4_s[:].rearrange("p a n -> p (a n)").bitcast(I32), 0)
         tab_w = []
         for a in range(PASSES):
             t = sb([P, T], U32, f"tab_w{a}", f"big{a}")
             nc.sync.dma_start(t[:].bitcast(I32), tab_words[a].rearrange("p t i -> p (t i)").bitcast(I32))
             tab_w.append(t)
-
         w4_hbm = w4_words.rearrange("a p n -> p a n")
         w4_first = sb([P, PASSES, 2 * P * FIRST], U8, "w4_first")
         nc.sync.dma_start(w4_first[:].bitcast(I32), w4_hbm[:, :, 0 : 2 * P * FIRST].bitcast(I32))
-        w4_s = sb([P, PASSES, H], U8, "w4_s")
-        nc.vector.memset(w4_s[:].rearrange("p a n -> p (a n)").bitcast(I32), 0)
+        wgs_sb = sb([P, S], F32, "wgs_sb")
+        nc.sync.dma_start(wgs_sb[:], wgs)
+        v_planes = sb([P, PASSES, S], U8, "v_planes")
+        nc.gpsimd.memset(v_planes[:].rearrange("p a n -> p (a n)").bitcast(I32), 0)
         for q in range(4):
-            nc.sync.dma_start(
+            nc.gpsimd.dma_start(
                 w4_s[32 * q : 32 * q + 4, :, :].bitcast(I32),
                 w4_scales[:, 4 * q : 4 * q + 4, :].rearrange("a r n -> r a n").bitcast(I32),
             )
-        wgs_sb = sb([P, S], F32, "wgs_sb")
-        nc.sync.dma_start(wgs_sb[:], wgs)
-        v_s1 = sb([P, S], U8, "v_s1")
-        nc.vector.memset(v_s1[:].bitcast(I32), 0)
 
         pages = [sb([P, T2], F32, f"page{i}") for i in range(2)]
-        nc.vector.memset(pages[0][:].bitcast(I32), 0)
-        nc.gpsimd.memset(pages[1][:].bitcast(I32), 0)
+        for page in pages:
+            nc.gpsimd.memset(page[:].bitcast(I32), 0)
 
         warm = sb([P, 8], F32, "warm")
-        nc.scalar.activation(warm[:, 0:1], pages[0][:, 0:1], SIGMOID)
+        nc.vector.memset(warm[:], 0.0)
+        nc.scalar.activation(warm[:, 1:2], warm[:, 0:1], SIGMOID)
 
         ident = keep.tile([P, P], F32, name="ident")
         make_identity(nc, ident[:])
 
-        v_s0 = sb([P, S], U8, "v_s0")
-        nc.vector.tensor_copy(v_s0[:], tab_s[:].indirect(list1[:]))
-        nc.scalar.dma_start(v_s1[0:112, :].bitcast(I32), v_s0[4:116, :].bitcast(I32))
-        v_s = [v_s0, v_s1]
+        v_rows = sb([P, S], U8, "v_rows")
+        nc.vector.tensor_copy(v_rows[:], tab_s[:].indirect(list1[:]))
+        for q in range(4):
+            nc.scalar.dma_start(
+                v_planes[32 * q : 32 * q + 4, :, :].bitcast(I32), v_rows[8 * q : 8 * q + 8, :].bitcast(I32)
+            )
+        v_s = [v_planes[:, a, :] for a in range(PASSES)]
+
 
         v_w = {}
         for a in range(PASSES):
@@ -102,7 +105,7 @@ def tile_list_beam_slot_gating_kernel(
         ifm_dealt = late[:, 4:8, :]
         wgs_dealt = late[:, 8:12, :]
         wv_raw = late[:, 12:16, :].rearrange("p (a x) m -> p a (x m)", a=2)
-        w4_rest = sb([P, PASSES, 2 * (H - P * FIRST)], U8, "w4_rest", "tab_s")
+        w4_rest = sb([P, PASSES, 2 * (H - P * FIRST)], U8, "w4_rest", "v_rows")
         nc.sync.dma_start(w4_rest[:].bitcast(I32), w4_hbm[:, :, 2 * P * FIRST : 2 * H].bitcast(I32))
         for k in range(2):
             nc.sync.dma_start(

@@ -23,7 +23,7 @@ PASSES = 2
 HALF = 512
 CHUNK = 256
 CHUNKS = M // CHUNK
-FIRST = 1
+FIRST = 2
 LAST_CUT = 768
 
 
@@ -74,7 +74,7 @@ def tile_list_beam_slot_gating_kernel(
             )
 
         pages = [sb([P, T2], F32, f"page{i}") for i in range(2)]
-        for page in pages:
+        for page in reversed(pages):
             nc.gpsimd.memset(page[:].bitcast(I32), 0)
 
         warm = sb([P, 8], F32, "warm")
@@ -94,11 +94,13 @@ def tile_list_beam_slot_gating_kernel(
 
 
         v_w = {}
-        for a in range(PASSES):
-            for jh in range(2):
-                t = sb([P, HALF], U32, f"v_w{a}{jh}")
-                nc.vector.tensor_copy(t[:], tab_w[a][:].indirect(list1[:, 32 * jh : 32 * jh + 32]))
-                v_w[(a, jh)] = t
+        v_w0 = sb([P, S], U32, "v_w0")
+        nc.vector.tensor_copy(v_w0[:], tab_w[0][:].indirect(list1[:]))
+        for jh in range(2):
+            v_w[(0, jh)] = v_w0[:, jh * HALF : (jh + 1) * HALF]
+            t = sb([P, HALF], U32, f"v_w1{jh}")
+            nc.vector.tensor_copy(t[:], tab_w[1][:].indirect(list1[:, 32 * jh : 32 * jh + 32]))
+            v_w[(1, jh)] = t[:]
 
         late = sb([P, 16, M], F32, "late", "big0")
         ifm_nat = late[:, 0:4, :]
@@ -130,16 +132,15 @@ def tile_list_beam_slot_gating_kernel(
                     out=bank[:],
                     lhsT=w4[:, a, c0 : c0 + 2 * P].bitcast(FP4X4),
                     lhsT_scale=w4_s[:, a, s * P : (s + 1) * P],
-                    rhs=v_w[(a, jh)][:].bitcast(FP8X4),
+                    rhs=v_w[(a, jh)].bitcast(FP8X4),
                     rhs_scale=v_s[a][:, jh * HALF : (jh + 1) * HALF],
                     start=(a == 0),
                     stop=(a == PASSES - 1),
                 )
             nc.scalar.copy(h[s][:, jh * HALF : (jh + 1) * HALF], bank[:])
 
-        for jh in range(2):
-            for s in range(2):
-                first_product(s, jh)
+        for s, jh in ((1, 0), (0, 0), (0, 1), (1, 1)):
+            first_product(s, jh)
         for s in range(2, 4):
             for jh in range(2):
                 first_product(s, jh)
@@ -175,7 +176,7 @@ def tile_list_beam_slot_gating_kernel(
             for dst, lo, hi in pieces:
                 nc.scalar.copy(dst, flat[:, lo:hi])
 
-        w8_w = sb([P, PASSES, N], U32, "w8_w", "v_w00")
+        w8_w = sb([P, PASSES, N], U32, "w8_w", "v_w0")
         nc.sync.dma_start(w8_w[:].bitcast(I32), w8_words.rearrange("a p n i -> p a (n i)").bitcast(I32))
         for q in range(4):
             nc.sync.dma_start(
@@ -194,10 +195,8 @@ def tile_list_beam_slot_gating_kernel(
         hp = {}
         for k in range(2):
             if k == 0:
-                for jh in range(2):
-                    for i in range(2):
-                        cols = slice(jh * HALF, (jh + 1) * HALF)
-                        scatter(pages[i], h[i][:, cols], wgs_sb[:, cols], jh * HALF, (jh + 1) * HALF)
+                for i, lo, hi in ((1, 0, HALF), (0, 0, S), (1, HALF, S)):
+                    scatter(pages[i], h[i][:, lo:hi], wgs_sb[:, lo:hi], lo, hi)
             else:
                 for i in range(2):
                     scatter(pages[i], h[2 + i][:], wgs_sb[:], 0, S)
@@ -256,7 +255,7 @@ def tile_list_beam_slot_gating_kernel(
         turn_plane(3, 1, [(hp3a[:, HALF:LAST_CUT], 0, LAST_CUT - HALF), (hp3b[:], LAST_CUT - HALF, HALF)])
         scatter(pages[0], hp[2][:], wgs_dealt[:, 2, :], 0, S)
         scatter(pages[1], hp3a[:], wgs_dealt[:, 3, 0:LAST_CUT], 0, LAST_CUT)
-        z0_w = sb([P, M], U32, "z0_w", "h2")
+        z0_w = sb([P, M], U32, "z0_w", "wv_bf")
         z0_s = sb([P, M], U8, "z0_s")
         nc.vector.quantize_mx(out=z0_w[:].bitcast(FP8X4), scales=z0_s[:], in_=z0_in[:].bitcast(BF16))
         scatter(pages[1], hp3b[:], wgs_dealt[:, 3, LAST_CUT:S], LAST_CUT, S)
@@ -315,8 +314,11 @@ def tile_list_beam_slot_gating_kernel(
             cols = slice(c * CHUNK, (c + 1) * CHUNK)
             gate = gates[(c, q)]
             res = sb([P, 2, CHUNK], F32, f"res{c}{q}", f"res{c % 2}{q}")
-            nc.vector.tensor_tensor(res[:], y_banks[(c, q, 1)][:], gate[:], MULT)
-            nc.sync.dma_start(out[256 * q : 256 * (q + 1), cols].rearrange("(i p) m -> p i m", i=2), res[:])
+            dst = out[256 * q : 256 * (q + 1), cols].rearrange("(i p) m -> p i m", i=2)
+            last = (c, q) == (CHUNKS - 1, 1)
+            for lo, hi in ((0, 1), (1, 2)) if last else ((0, 2),):
+                nc.vector.tensor_tensor(res[:, lo:hi, :], y_banks[(c, q, 1)][:, lo:hi, :], gate[:, lo:hi, :], MULT)
+                nc.sync.dma_start(dst[:, lo:hi, :], res[:, lo:hi, :])
 
         for c in range(2):
             for q in range(2):

@@ -25,6 +25,7 @@ CHUNK = 256
 CHUNKS = M // CHUNK
 FIRST = 2
 LAST_CUT = 768
+LEAD = 256
 
 
 def tile_list_beam_slot_gating_kernel(
@@ -63,8 +64,8 @@ def tile_list_beam_slot_gating_kernel(
         w4_hbm = w4_words.rearrange("a p n -> p a n")
         w4_first = sb([P, PASSES, 2 * P * FIRST], U8, "w4_first")
         nc.sync.dma_start(w4_first[:].bitcast(I32), w4_hbm[:, :, 0 : 2 * P * FIRST].bitcast(I32))
-        wgs_sb = sb([P, S], F32, "wgs_sb")
-        nc.sync.dma_start(wgs_sb[:], wgs)
+        wgs_lead = sb([P, LEAD], F32, "wgs_lead")
+        nc.sync.dma_start(wgs_lead[:], wgs[:, 0:LEAD])
         v_planes = sb([P, PASSES, S], U8, "v_planes")
         nc.gpsimd.memset(v_planes[:].rearrange("p a n -> p (a n)").bitcast(I32), 0)
         for q in range(4):
@@ -74,7 +75,7 @@ def tile_list_beam_slot_gating_kernel(
             )
 
         pages = [sb([P, T2], F32, f"page{i}") for i in range(2)]
-        for page in reversed(pages):
+        for page in pages:
             nc.gpsimd.memset(page[:].bitcast(I32), 0)
 
         warm = sb([P, 8], F32, "warm")
@@ -93,16 +94,13 @@ def tile_list_beam_slot_gating_kernel(
         v_s = [v_planes[:, a, :] for a in range(PASSES)]
 
 
-        v_w = {}
-        v_w0 = sb([P, S], U32, "v_w0")
-        nc.vector.tensor_copy(v_w0[:], tab_w[0][:].indirect(list1[:]))
-        for jh in range(2):
-            v_w[(0, jh)] = v_w0[:, jh * HALF : (jh + 1) * HALF]
-            t = sb([P, HALF], U32, f"v_w1{jh}")
-            nc.vector.tensor_copy(t[:], tab_w[1][:].indirect(list1[:, 32 * jh : 32 * jh + 32]))
-            v_w[(1, jh)] = t[:]
+        v_w = [sb([P, S], U32, f"v_w{a}") for a in range(PASSES)]
+        for a, lo, hi in ((0, 0, S), (1, 0, LEAD), (1, LEAD, S)):
+            nc.vector.tensor_copy(v_w[a][:, lo:hi], tab_w[a][:].indirect(list1[:, lo // 16 : hi // 16]))
 
-        late = sb([P, 16, M], F32, "late", "big0")
+        late = sb([P, 17, M], F32, "late", "big0")
+        wgs_sb = late[:, 16, :]
+        nc.sync.dma_start(wgs_sb, wgs)
         ifm_nat = late[:, 0:4, :]
         ifm_dealt = late[:, 4:8, :]
         wgs_dealt = late[:, 8:12, :]
@@ -123,27 +121,30 @@ def tile_list_beam_slot_gating_kernel(
 
         h = [sb([P, S], F32, f"h{s}") for s in range(4)]
 
-        def first_product(s, jh):
-            bank = bank_tile([P, HALF], f"h_bank{s}{jh}", 2 * jh + s % 2)
+        def first_product(s, lo, hi, index):
+            bank = bank_tile([P, hi - lo], f"h_bank{s}_{lo}", index)
             w4 = w4_first if s < FIRST else w4_rest
             c0 = 2 * P * (s if s < FIRST else s - FIRST)
-            for a in range(PASSES):
-                nc.tensor.matmul_mx(
-                    out=bank[:],
-                    lhsT=w4[:, a, c0 : c0 + 2 * P].bitcast(FP4X4),
-                    lhsT_scale=w4_s[:, a, s * P : (s + 1) * P],
-                    rhs=v_w[(a, jh)].bitcast(FP8X4),
-                    rhs_scale=v_s[a][:, jh * HALF : (jh + 1) * HALF],
-                    start=(a == 0),
-                    stop=(a == PASSES - 1),
-                )
-            nc.scalar.copy(h[s][:, jh * HALF : (jh + 1) * HALF], bank[:])
+            width = HALF if hi - lo == HALF else P
+            for j0 in range(lo, hi, width):
+                for a in range(PASSES):
+                    nc.tensor.matmul_mx(
+                        out=bank[:, j0 - lo : j0 - lo + width],
+                        lhsT=w4[:, a, c0 : c0 + 2 * P].bitcast(FP4X4),
+                        lhsT_scale=w4_s[:, a, s * P : (s + 1) * P],
+                        rhs=v_w[a][:, j0 : j0 + width].bitcast(FP8X4),
+                        rhs_scale=v_s[a][:, j0 : j0 + width],
+                        start=(a == 0),
+                        stop=(a == PASSES - 1),
+                    )
+            nc.scalar.copy(h[s][:, lo:hi], bank[:])
 
-        for s, jh in ((1, 0), (0, 0), (0, 1), (1, 1)):
-            first_product(s, jh)
+        for piece, (lo, hi) in enumerate(((0, LEAD), (LEAD, HALF), (HALF, S))):
+            for s in range(2):
+                first_product(s, lo, hi, 2 * piece + s)
         for s in range(2, 4):
             for jh in range(2):
-                first_product(s, jh)
+                first_product(s, jh * HALF, (jh + 1) * HALF, 2 * jh + s % 2)
 
         h_t = [sb([P, 4, 4, P], F32, f"h_t{jh}", ("h_t0", "big1")[jh]) for jh in range(2)]
         c_hi = 2 * (HALF - P * FIRST)
@@ -154,7 +155,7 @@ def tile_list_beam_slot_gating_kernel(
                 for a in range(PASSES):
                     nc.tensor.matmul_mx(
                         out=bank[:],
-                        lhsT=v_w[(a, jh)][:, i * P : (i + 1) * P].bitcast(FP8X4),
+                        lhsT=v_w[a][:, j0 : j0 + P].bitcast(FP8X4),
                         lhsT_scale=v_s[a][:, j0 : j0 + P],
                         rhs=w4_rest[:, a, c_hi : c_hi + 2 * HALF].bitcast(FP4X4),
                         rhs_scale=w4_s[:, a, HALF:H],
@@ -195,11 +196,13 @@ def tile_list_beam_slot_gating_kernel(
         hp = {}
         for k in range(2):
             if k == 0:
-                for i, lo, hi in ((1, 0, HALF), (0, 0, S), (1, HALF, S)):
-                    scatter(pages[i], h[i][:, lo:hi], wgs_sb[:, lo:hi], lo, hi)
+                for i in range(2):
+                    scatter(pages[i], h[i][:, 0:LEAD], wgs_lead[:], 0, LEAD)
+                for i in range(2):
+                    scatter(pages[i], h[i][:, LEAD:S], wgs_sb[:, LEAD:S], LEAD, S)
             else:
                 for i in range(2):
-                    scatter(pages[i], h[2 + i][:], wgs_sb[:], 0, S)
+                    scatter(pages[i], h[2 + i][:], wgs_sb, 0, S)
             x = sb([P, 2, M], F32, f"x{k}")
             for i in range(2):
                 gather(x[:, i, :], pages[i], ifm_nat[:, 2 * k + i, :], 0, M)

@@ -75,8 +75,9 @@ def tile_list_beam_slot_gating_kernel(
             )
 
         pages = [sb([P, T2], F32, f"page{i}") for i in range(2)]
-        for page in pages:
-            nc.gpsimd.memset(page[:].bitcast(I32), 0)
+        nc.vector.memset(pages[0][:].bitcast(I32), 0)
+        nc.vector.memset(pages[1][:, 0 : T2 // 2].bitcast(I32), 0)
+        nc.gpsimd.memset(pages[1][:, T2 // 2 : T2].bitcast(I32), 0)
 
         warm = sb([P, 8], F32, "warm")
         nc.vector.memset(warm[:], 0.0)

@@ -259,9 +259,17 @@ def tile_list_beam_slot_gating_kernel(
         turn_plane(3, 1, [(hp3a[:, HALF:LAST_CUT], 0, LAST_CUT - HALF), (hp3b[:], LAST_CUT - HALF, HALF)])
         scatter(pages[0], hp[2][:], wgs_dealt[:, 2, :], 0, S)
         scatter(pages[1], hp3a[:], wgs_dealt[:, 3, 0:LAST_CUT], 0, LAST_CUT)
-        z0_w = sb([P, M], U32, "z0_w", "wv_bf")
-        z0_s = sb([P, M], U8, "z0_s")
-        nc.vector.quantize_mx(out=z0_w[:].bitcast(FP8X4), scales=z0_s[:], in_=z0_in[:].bitcast(BF16))
+        z0 = {}
+
+        def quantise_z0(half, tag):
+            z0_w = sb([P, HALF], U32, f"z0_w{half}", tag)
+            z0_s = sb([P, HALF], U8, f"z0_s{half}")
+            nc.vector.quantize_mx(
+                out=z0_w[:].bitcast(FP8X4), scales=z0_s[:], in_=z0_in[:, half * M : (half + 1) * M].bitcast(BF16)
+            )
+            z0[half] = (z0_w, z0_s)
+
+        quantise_z0(0, "wv_bf")
         scatter(pages[1], hp3b[:], wgs_dealt[:, 3, LAST_CUT:S], LAST_CUT, S)
 
         z1 = {}
@@ -271,7 +279,7 @@ def tile_list_beam_slot_gating_kernel(
 
         def late_gathers(c):
             cols = slice(c * CHUNK, (c + 1) * CHUNK)
-            xc[c] = sb([P, 2, CHUNK], F32, f"xc{c}", f"xc{c % 2}")
+            xc[c] = sb([P, 2, CHUNK], F32, f"xc{c}", ("xc0", "xc1", "zt0", "xc1")[c])
             for i in range(2):
                 gather(xc[c][:, i, :], pages[i], ifm_dealt[:, 2 + i, cols], c * CHUNK, (c + 1) * CHUNK)
 
@@ -287,10 +295,10 @@ def tile_list_beam_slot_gating_kernel(
             z1[c] = (z1_w, z1_s)
 
         def second_pass(c, q, w, a):
-            cols = slice(c * CHUNK, (c + 1) * CHUNK)
             if a == 0:
                 y_banks[(c, q, w)] = bank_tile([P, 2, CHUNK], f"Y{c}{q}{w}", 4 * (c % 2) + 2 * q + w)
-                z_w, z_s = z0_w[:, cols], z0_s[:, cols]
+                part = slice((c % 2) * CHUNK, (c % 2 + 1) * CHUNK)
+                z_w, z_s = z0[c // 2][0][:, part], z0[c // 2][1][:, part]
             else:
                 z_w, z_s = z1[c][0][:], z1[c][1][:]
             w_w, w_s, row = ((w8_w, w4_s, 4), (wv_w, wv_s, 0))[w]
@@ -332,6 +340,7 @@ def tile_list_beam_slot_gating_kernel(
             late_gathers(c)
             weave(c)
         quantise_z1(0)
+        quantise_z0(1, "xc0")
         for c in range(CHUNKS):
             if c + 2 < CHUNKS:
                 late_gathers(c + 2)

@@ -34,6 +34,8 @@ def tile_list_beam_slot_gating_kernel(
     nc = tc.nc
     with ExitStack() as ctx:
         keep = ctx.enter_context(tc.tile_pool(name="keep", bufs=1))
+        head = ctx.enter_context(tc.tile_pool(name="head", bufs=1))
+        stage = ctx.enter_context(tc.tile_pool(name="stage", bufs=1))
         psum = ctx.enter_context(tc.psum_pool(name="psum", bufs=1))
 
         def sb(shape, dtype, name, tag=None):
@@ -47,37 +49,34 @@ def tile_list_beam_slot_gating_kernel(
         list3 = keep.tile([P, M // 16], U16, name="list3")
         nc.sync.dma_start(list1[:], offs)
 
-        tab_s = sb([P, T], U8, "tab_s")
+        tab_s = head.tile([P, T], U8, name="tab_s", offset=0, align_bytes=64)
         nc.sync.dma_start(tab_s[0:32, :].bitcast(I32), tab_scales.rearrange("a q t -> q a t").bitcast(I32))
         nc.vector.memset(tab_s[32:64, :].bitcast(I32), 0)
         nc.vector.memset(tab_s[64:P, :].bitcast(I32), 0)
-        nc.sync.dma_start(list2[:], offs2)
-        nc.sync.dma_start(list3[:], offs3)
 
-        w4_s = sb([P, PASSES, H], U8, "w4_s")
-        nc.gpsimd.memset(w4_s[:].rearrange("p a n -> p (a n)").bitcast(I32), 0)
+        w4_s_first = sb([P, PASSES, P * FIRST], U8, "w4_s_first")
+        nc.gpsimd.memset(w4_s_first[:].rearrange("p a n -> p (a n)").bitcast(I32), 0)
         tab_w = []
         for a in range(PASSES):
-            t = sb([P, T], U32, f"tab_w{a}", f"big{a}")
+            if a == 0:
+                t = stage.tile([P, T], U32, name="tab_w0", offset=0, align_bytes=64)
+            else:
+                t = sb([P, T], U32, "tab_w1", "big1")
             nc.sync.dma_start(t[:].bitcast(I32), tab_words[a].rearrange("p t i -> p (t i)").bitcast(I32))
             tab_w.append(t)
-        w4_hbm = w4_words.rearrange("a p n -> p a n")
-        w4_first = sb([P, PASSES, 2 * P * FIRST], U8, "w4_first")
-        nc.sync.dma_start(w4_first[:].bitcast(I32), w4_hbm[:, :, 0 : 2 * P * FIRST].bitcast(I32))
-        wgs_lead = sb([P, LEAD], F32, "wgs_lead")
-        nc.sync.dma_start(wgs_lead[:], wgs[:, 0:LEAD])
+        nc.sync.dma_start(list2[:], offs2)
+        nc.sync.dma_start(list3[:], offs3)
         v_planes = sb([P, PASSES, S], U8, "v_planes")
         nc.gpsimd.memset(v_planes[:].rearrange("p a n -> p (a n)").bitcast(I32), 0)
         for q in range(4):
             nc.gpsimd.dma_start(
-                w4_s[32 * q : 32 * q + 4, :, :].bitcast(I32),
-                w4_scales[:, 4 * q : 4 * q + 4, :].rearrange("a r n -> r a n").bitcast(I32),
+                w4_s_first[32 * q : 32 * q + 4, :, :].bitcast(I32),
+                w4_scales[:, 4 * q : 4 * q + 4, 0 : P * FIRST].rearrange("a r n -> r a n").bitcast(I32),
             )
 
         pages = [sb([P, T2], F32, f"page{i}") for i in range(2)]
         nc.vector.memset(pages[0][:].bitcast(I32), 0)
-        nc.vector.memset(pages[1][:, 0 : T2 // 2].bitcast(I32), 0)
-        nc.gpsimd.memset(pages[1][:, T2 // 2 : T2].bitcast(I32), 0)
+        nc.gpsimd.memset(pages[1][:].bitcast(I32), 0)
 
         warm = sb([P, 8], F32, "warm")
         nc.vector.memset(warm[:], 0.0)
@@ -93,13 +92,20 @@ def tile_list_beam_slot_gating_kernel(
                 v_planes[32 * q : 32 * q + 4, :, :].bitcast(I32), v_rows[8 * q : 8 * q + 8, :].bitcast(I32)
             )
         v_s = [v_planes[:, a, :] for a in range(PASSES)]
+        w4_hbm = w4_words.rearrange("a p n -> p a n")
+        w4_first = head.tile([P, PASSES, 2 * P * FIRST], U8, name="w4_first", offset=0, align_bytes=64)
+        nc.sync.dma_start(w4_first[:].bitcast(I32), w4_hbm[:, :, 0 : 2 * P * FIRST].bitcast(I32))
+        wgs_lead = head.tile([P, LEAD], F32, name="wgs_lead", offset=T // 2, align_bytes=64)
+        nc.sync.dma_start(wgs_lead[:], wgs[:, 0:LEAD])
 
 
         v_w = [sb([P, S], U32, f"v_w{a}") for a in range(PASSES)]
         for a, lo, hi in ((0, 0, S), (1, 0, LEAD), (1, LEAD, S)):
             nc.vector.tensor_copy(v_w[a][:, lo:hi], tab_w[a][:].indirect(list1[:, lo // 16 : hi // 16]))
 
-        late = sb([P, 17, M], F32, "late", "big0")
+        w4_s = stage.tile([P, PASSES, H], U8, name="w4_s", offset=0, align_bytes=64)
+        nc.gpsimd.memset(w4_s[:].rearrange("p a n -> p (a n)").bitcast(I32), 0)
+        late = stage.tile([P, 17, M], F32, name="late", offset=PASSES * H, align_bytes=64)
         wgs_sb = late[:, 16, :]
         nc.sync.dma_start(wgs_sb, wgs)
         ifm_nat = late[:, 0:4, :]
@@ -108,6 +114,11 @@ def tile_list_beam_slot_gating_kernel(
         wv_raw = late[:, 12:16, :].rearrange("p (a x) m -> p a (x m)", a=2)
         w4_rest = sb([P, PASSES, 2 * (H - P * FIRST)], U8, "w4_rest", "v_rows")
         nc.sync.dma_start(w4_rest[:].bitcast(I32), w4_hbm[:, :, 2 * P * FIRST : 2 * H].bitcast(I32))
+        for q in range(4):
+            nc.sync.dma_start(
+                w4_s[32 * q : 32 * q + 4, :, P * FIRST : H].bitcast(I32),
+                w4_scales[:, 4 * q : 4 * q + 4, P * FIRST : H].rearrange("a r n -> r a n").bitcast(I32),
+            )
         for k in range(2):
             nc.sync.dma_start(
                 ifm_nat[:, 2 * k : 2 * k + 2, :], ifm[256 * k : 256 * (k + 1), :].rearrange("(s p) m -> p s m", s=2)
@@ -132,7 +143,7 @@ def tile_list_beam_slot_gating_kernel(
                     nc.tensor.matmul_mx(
                         out=bank[:, j0 - lo : j0 - lo + width],
                         lhsT=w4[:, a, c0 : c0 + 2 * P].bitcast(FP4X4),
-                        lhsT_scale=w4_s[:, a, s * P : (s + 1) * P],
+                        lhsT_scale=(w4_s_first if s < FIRST else w4_s)[:, a, s * P : (s + 1) * P],
                         rhs=v_w[a][:, j0 : j0 + width].bitcast(FP8X4),
                         rhs_scale=v_s[a][:, j0 : j0 + width],
                         start=(a == 0),

@@ -64,26 +64,26 @@ def tile_list_beam_slot_gating_kernel(
                 t = sb([P, T], U32, "tab_w1", "big1")
             nc.sync.dma_start(t[:].bitcast(I32), tab_words[a].rearrange("p t i -> p (t i)").bitcast(I32))
             tab_w.append(t)
+        w4_hbm = w4_words.rearrange("a p n -> p a n")
+        w4_first = sb([P, PASSES, 2 * P * FIRST], U8, "w4_first")
+        nc.sync.dma_start(w4_first[:].bitcast(I32), w4_hbm[:, :, 0 : 2 * P * FIRST].bitcast(I32))
         nc.sync.dma_start(list2[:], offs2)
         nc.sync.dma_start(list3[:], offs3)
         v_planes = sb([P, PASSES, S], U8, "v_planes")
-        nc.gpsimd.memset(v_planes[:].rearrange("p a n -> p (a n)").bitcast(I32), 0)
+        nc.vector.memset(v_planes[:].rearrange("p a n -> p (a n)").bitcast(I32), 0)
         for q in range(4):
             nc.gpsimd.dma_start(
                 w4_s_first[32 * q : 32 * q + 4, :, :].bitcast(I32),
                 w4_scales[:, 4 * q : 4 * q + 4, 0 : P * FIRST].rearrange("a r n -> r a n").bitcast(I32),
             )
 
-        pages = [sb([P, T2], F32, f"page{i}") for i in range(2)]
+        pages = [sb([P, T2], F32, "page0")]
         nc.vector.memset(pages[0][:].bitcast(I32), 0)
-        nc.gpsimd.memset(pages[1][:].bitcast(I32), 0)
 
         warm = sb([P, 8], F32, "warm")
         nc.vector.memset(warm[:], 0.0)
         nc.scalar.activation(warm[:, 1:2], warm[:, 0:1], SIGMOID)
 
-        ident = keep.tile([P, P], F32, name="ident")
-        make_identity(nc, ident[:])
 
         v_rows = sb([P, S], U8, "v_rows")
         nc.vector.tensor_copy(v_rows[:], tab_s[:].indirect(list1[:]))
@@ -92,11 +92,12 @@ def tile_list_beam_slot_gating_kernel(
                 v_planes[32 * q : 32 * q + 4, :, :].bitcast(I32), v_rows[8 * q : 8 * q + 8, :].bitcast(I32)
             )
         v_s = [v_planes[:, a, :] for a in range(PASSES)]
-        w4_hbm = w4_words.rearrange("a p n -> p a n")
-        w4_first = head.tile([P, PASSES, 2 * P * FIRST], U8, name="w4_first", offset=0, align_bytes=64)
-        nc.sync.dma_start(w4_first[:].bitcast(I32), w4_hbm[:, :, 0 : 2 * P * FIRST].bitcast(I32))
-        wgs_lead = head.tile([P, LEAD], F32, name="wgs_lead", offset=T // 2, align_bytes=64)
+        wgs_lead = head.tile([P, LEAD], F32, name="wgs_lead", offset=0, align_bytes=64)
         nc.sync.dma_start(wgs_lead[:], wgs[:, 0:LEAD])
+        pages.append(head.tile([P, T2], F32, name="page1", offset=4 * LEAD + 4 * P, align_bytes=64))
+        nc.gpsimd.memset(pages[1][:].bitcast(I32), 0)
+        ident = head.tile([P, P], F32, name="ident", offset=4 * LEAD, align_bytes=64)
+        make_identity(nc, ident[:])
 
 
         v_w = [sb([P, S], U32, f"v_w{a}") for a in range(PASSES)]
@@ -104,7 +105,6 @@ def tile_list_beam_slot_gating_kernel(
             nc.vector.tensor_copy(v_w[a][:, lo:hi], tab_w[a][:].indirect(list1[:, lo // 16 : hi // 16]))
 
         w4_s = stage.tile([P, PASSES, H], U8, name="w4_s", offset=0, align_bytes=64)
-        nc.gpsimd.memset(w4_s[:].rearrange("p a n -> p (a n)").bitcast(I32), 0)
         late = stage.tile([P, 17, M], F32, name="late", offset=PASSES * H, align_bytes=64)
         wgs_sb = late[:, 16, :]
         nc.sync.dma_start(wgs_sb, wgs)
@@ -138,22 +138,24 @@ def tile_list_beam_slot_gating_kernel(
             w4 = w4_first if s < FIRST else w4_rest
             c0 = 2 * P * (s if s < FIRST else s - FIRST)
             width = HALF if hi - lo == HALF else P
-            for j0 in range(lo, hi, width):
-                for a in range(PASSES):
+            for a in range(PASSES):
+                for j0 in range(lo, hi, width):
                     nc.tensor.matmul_mx(
                         out=bank[:, j0 - lo : j0 - lo + width],
                         lhsT=w4[:, a, c0 : c0 + 2 * P].bitcast(FP4X4),
                         lhsT_scale=(w4_s_first if s < FIRST else w4_s)[:, a, s * P : (s + 1) * P],
                         rhs=v_w[a][:, j0 : j0 + width].bitcast(FP8X4),
                         rhs_scale=v_s[a][:, j0 : j0 + width],
-                        start=(a == 0),
-                        stop=(a == PASSES - 1),
+                        start=(a == 0 and j0 == lo),
+                        stop=(a == PASSES - 1 and j0 + width == hi),
                     )
             nc.scalar.copy(h[s][:, lo:hi], bank[:])
 
-        for piece, (lo, hi) in enumerate(((0, LEAD), (LEAD, HALF), (HALF, S))):
-            for s in range(2):
-                first_product(s, lo, hi, 2 * piece + s)
+        for s in range(2):
+            first_product(s, 0, LEAD, s)
+        for s in range(2):
+            first_product(s, LEAD, LEAD + HALF, 0)
+            first_product(s, LEAD + HALF, S, 1)
         for s in range(2, 4):
             for jh in range(2):
                 first_product(s, jh * HALF, (jh + 1) * HALF, 2 * jh + s % 2)

@@ -340,10 +340,8 @@ def tile_list_beam_slot_gating_kernel(
             gate = gates[(c, q)]
             res = sb([P, 2, CHUNK], F32, f"res{c}{q}", f"res{c % 2}{q}")
             dst = out[256 * q : 256 * (q + 1), cols].rearrange("(i p) m -> p i m", i=2)
-            last = (c, q) == (CHUNKS - 1, 1)
-            for lo, hi in ((0, 1), (1, 2)) if last else ((0, 2),):
-                nc.vector.tensor_tensor(res[:, lo:hi, :], y_banks[(c, q, 1)][:, lo:hi, :], gate[:, lo:hi, :], MULT)
-                nc.sync.dma_start(dst[:, lo:hi, :], res[:, lo:hi, :])
+            nc.vector.tensor_tensor(res[:], y_banks[(c, q, 1)][:], gate[:], MULT)
+            nc.sync.dma_start(dst, res[:])
 
         for c in range(2):
             for q in range(2):

@@ -86,11 +86,13 @@ def tile_list_beam_slot_gating_kernel(
 
 
         v_rows = sb([P, S], U8, "v_rows")
-        nc.vector.tensor_copy(v_rows[:], tab_s[:].indirect(list1[:]))
-        for q in range(4):
-            nc.scalar.dma_start(
-                v_planes[32 * q : 32 * q + 4, :, :].bitcast(I32), v_rows[8 * q : 8 * q + 8, :].bitcast(I32)
-            )
+        for lo, hi in ((0, LEAD), (LEAD, S)):
+            nc.vector.tensor_copy(v_rows[:, lo:hi], tab_s[:].indirect(list1[:, lo // 16 : hi // 16]))
+            for q in range(4):
+                nc.scalar.dma_start(
+                    v_planes[32 * q : 32 * q + 4, :, lo:hi].bitcast(I32),
+                    v_rows[8 * q : 8 * q + 8, lo:hi].bitcast(I32),
+                )
         v_s = [v_planes[:, a, :] for a in range(PASSES)]
         wgs_lead = head.tile([P, LEAD], F32, name="wgs_lead", offset=0, align_bytes=64)
         nc.sync.dma_start(wgs_lead[:], wgs[:, 0:LEAD])

@@ -24,7 +24,6 @@ HALF = 512
 CHUNK = 256
 CHUNKS = M // CHUNK
 FIRST = 2
-LAST_CUT = 768
 LEAD = 256
 
 
@@ -36,6 +35,7 @@ def tile_list_beam_slot_gating_kernel(
         keep = ctx.enter_context(tc.tile_pool(name="keep", bufs=1))
         head = ctx.enter_context(tc.tile_pool(name="head", bufs=1))
         stage = ctx.enter_context(tc.tile_pool(name="stage", bufs=1))
+        third = ctx.enter_context(tc.tile_pool(name="third", bufs=1))
         psum = ctx.enter_context(tc.psum_pool(name="psum", bufs=1))
 
         def sb(shape, dtype, name, tag=None):
@@ -65,7 +65,7 @@ def tile_list_beam_slot_gating_kernel(
             nc.sync.dma_start(t[:].bitcast(I32), tab_words[a].rearrange("p t i -> p (t i)").bitcast(I32))
             tab_w.append(t)
         w4_hbm = w4_words.rearrange("a p n -> p a n")
-        w4_first = sb([P, PASSES, 2 * P * FIRST], U8, "w4_first")
+        w4_first = third.tile([P, PASSES, 2 * P * FIRST], U8, name="w4_first", offset=0, align_bytes=64)
         nc.sync.dma_start(w4_first[:].bitcast(I32), w4_hbm[:, :, 0 : 2 * P * FIRST].bitcast(I32))
         nc.sync.dma_start(list2[:], offs2)
         nc.sync.dma_start(list3[:], offs3)
@@ -255,25 +255,22 @@ def tile_list_beam_slot_gating_kernel(
             in_=wv_tile[:],
         )
 
-        for t in range(2):
-            scatter(pages[t], hp[t][:], wgs_dealt[:, t, :], 0, S)
-        x01 = sb([P, 2, M], F32, "x01", "x0")
-        for t in range(2):
-            gather(x01[:, t, :], pages[t], ifm_dealt[:, t, :], 0, M)
+        pages.append(third.tile([P, T2], F32, name="page2", offset=0, align_bytes=64))
+        nc.gpsimd.memset(pages[2][:].bitcast(I32), 0)
+        scatter(pages[2], hp[0][:], wgs_dealt[:, 0, :], 0, S)
+        scatter(pages[0], hp[1][:], wgs_dealt[:, 1, :], 0, S)
+        x_plane0 = sb([P, M], F32, "x_plane0", "x0")
+        gather(x_plane0[:], pages[2], ifm_dealt[:, 0, :], 0, M)
         z1_in = [sb([P, CHUNK, 4], BF16, f"z1_in{c}", f"zt{c}") for c in range(CHUNKS)]
         for c in range(CHUNKS):
-            cols = slice(c * CHUNK, (c + 1) * CHUNK)
-            nc.scalar.copy(z1_in[c][:, :, 0:2], x01[:, :, cols].rearrange("p e m -> p m e"))
+            nc.scalar.copy(z1_in[c][:, :, 0], x_plane0[:, c * CHUNK : (c + 1) * CHUNK])
 
         hp[2] = sb([P, S], F32, "hp2", "wv_bf")
-        for jh in range(2):
-            turn_plane(2, jh, [(hp[2][:, jh * HALF : (jh + 1) * HALF], 0, HALF)])
-        hp3a = sb([P, LAST_CUT], F32, "hp3a", "h2")
-        hp3b = sb([P, S - LAST_CUT], F32, "hp3b", "h3")
-        turn_plane(3, 0, [(hp3a[:, 0:HALF], 0, HALF)])
-        turn_plane(3, 1, [(hp3a[:, HALF:LAST_CUT], 0, LAST_CUT - HALF), (hp3b[:], LAST_CUT - HALF, HALF)])
-        scatter(pages[0], hp[2][:], wgs_dealt[:, 2, :], 0, S)
-        scatter(pages[1], hp3a[:], wgs_dealt[:, 3, 0:LAST_CUT], 0, LAST_CUT)
+        hp[3] = sb([P, S], F32, "hp3", "h2")
+        for t in range(2, 4):
+            for jh in range(2):
+                turn_plane(t, jh, [(hp[t][:, jh * HALF : (jh + 1) * HALF], 0, HALF)])
+            scatter(pages[t - 1], hp[t][:], wgs_dealt[:, t, :], 0, S)
         z0 = {}
 
         def quantise_z0(half, tag):
@@ -285,7 +282,6 @@ def tile_list_beam_slot_gating_kernel(
             z0[half] = (z0_w, z0_s)
 
         quantise_z0(0, "wv_bf")
-        scatter(pages[1], hp3b[:], wgs_dealt[:, 3, LAST_CUT:S], LAST_CUT, S)
 
         z1 = {}
         xc = {}
@@ -294,12 +290,15 @@ def tile_list_beam_slot_gating_kernel(
 
         def late_gathers(c):
             cols = slice(c * CHUNK, (c + 1) * CHUNK)
-            xc[c] = sb([P, 2, CHUNK], F32, f"xc{c}", ("xc0", "xc1", "zt0", "xc1")[c])
-            for i in range(2):
-                gather(xc[c][:, i, :], pages[i], ifm_dealt[:, 2 + i, cols], c * CHUNK, (c + 1) * CHUNK)
+            xc[c] = sb([P, 3, CHUNK], F32, f"xc{c}", ("xc0", "xc1", "zt0", "xc1")[c])
+            for i in range(3):
+                gather(xc[c][:, i, :], pages[i], ifm_dealt[:, 1 + i, cols], c * CHUNK, (c + 1) * CHUNK)
 
         def weave(c):
-            nc.scalar.copy(z1_in[c][:, :, 2:4], xc[c][:].rearrange("p e m -> p m e"))
+            nc.scalar.copy(
+                z1_in[c][:, :, 1:4].rearrange("p (g i) t -> p g t i", i=4),
+                xc[c][:].rearrange("p t (g i) -> p g t i", i=4),
+            )
 
         def quantise_z1(c):
             z1_w = sb([P, CHUNK], U32, f"z1_w{c}")
@@ -309,61 +308,89 @@ def tile_list_beam_slot_gating_kernel(
             )
             z1[c] = (z1_w, z1_s)
 
-        def second_pass(c, q, w, a):
+        def mx_pass(dst, nb, w, a, z_w, z_s, start, stop):
+            w_w, w_s, row = ((w8_w, w4_s, 4), (wv_w, wv_s, 0))[w]
+            nc.tensor.matmul_mx(
+                out=dst,
+                lhsT=w_w[:, a, nb * P : (nb + 1) * P].bitcast(FP8X4),
+                lhsT_scale=w_s[row:P, a, nb * P : (nb + 1) * P],
+                rhs=z_w.bitcast(FP8X4),
+                rhs_scale=z_s,
+                start=start,
+                stop=stop,
+            )
+
+        def sigmoid(key, slot):
+            gates[key] = sb([P, HALF], F32, f"gate{key[0]}{key[1]}", f"gate{slot}")
+            nc.scalar.activation(gates[key][:], y_banks[key + (0,)][:], SIGMOID)
+
+        def early_pass(c, q, w, a):
             if a == 0:
-                y_banks[(c, q, w)] = bank_tile([P, 2, CHUNK], f"Y{c}{q}{w}", 4 * (c % 2) + 2 * q + w)
-                part = slice((c % 2) * CHUNK, (c % 2 + 1) * CHUNK)
-                z_w, z_s = z0[c // 2][0][:, part], z0[c // 2][1][:, part]
+                y_banks[(c, q, w)] = bank_tile([P, HALF], f"Y{c}{q}{w}", 4 * c + 2 * q + w)
+                part = slice(c * CHUNK, (c + 1) * CHUNK)
+                z_w, z_s = z0[0][0][:, part], z0[0][1][:, part]
             else:
                 z_w, z_s = z1[c][0][:], z1[c][1][:]
-            w_w, w_s, row = ((w8_w, w4_s, 4), (wv_w, wv_s, 0))[w]
             for i in range(2):
-                n0 = (2 * q + i) * P
-                nc.tensor.matmul_mx(
-                    out=y_banks[(c, q, w)][:, i, :],
-                    lhsT=w_w[:, a, n0 : n0 + P].bitcast(FP8X4),
-                    lhsT_scale=w_s[row:P, a, n0 : n0 + P],
-                    rhs=z_w.bitcast(FP8X4),
-                    rhs_scale=z_s,
-                    start=(a == 0 and i == 0),
-                    stop=(a == PASSES - 1 and i == 1),
-                )
+                dst = y_banks[(c, q, w)][:, i * CHUNK : (i + 1) * CHUNK]
+                mx_pass(dst, 2 * q + i, w, a, z_w, z_s, a == 0 and i == 0, a == 1 and i == 1)
+            if a == 1 and w == 0:
+                sigmoid((c, q), 2 * c + q)
 
-        def products(c, q):
-            for w in range(2):
-                if (c, q, w) not in y_banks:
-                    second_pass(c, q, w, 0)
-                second_pass(c, q, w, 1)
-            gates[(c, q)] = sb([P, 2, CHUNK], F32, f"gate{c}{q}", f"gate{c % 2}{q}")
-            nc.scalar.activation(gates[(c, q)][:], y_banks[(c, q, 0)][:], SIGMOID)
+        def open_late(nb, w):
+            y_banks[(2, nb, w)] = bank_tile([P, HALF], f"Y2{nb}{w}", 2 * nb + w)
+            mx_pass(y_banks[(2, nb, w)][:], nb, w, 0, z0[1][0][:], z0[1][1][:], True, False)
 
-        def finish(c, q):
-            cols = slice(c * CHUNK, (c + 1) * CHUNK)
-            gate = gates[(c, q)]
-            res = sb([P, 2, CHUNK], F32, f"res{c}{q}", f"res{c % 2}{q}")
-            dst = out[256 * q : 256 * (q + 1), cols].rearrange("(i p) m -> p i m", i=2)
-            nc.vector.tensor_tensor(res[:], y_banks[(c, q, 1)][:], gate[:], MULT)
-            nc.sync.dma_start(dst, res[:])
+        def add_late(c, nb, w):
+            dst = y_banks[(2, nb, w)][:, (c - 2) * CHUNK : (c - 1) * CHUNK]
+            mx_pass(dst, nb, w, 1, z1[c][0][:], z1[c][1][:], False, c == 3)
+            if c == 3 and w == 0:
+                sigmoid((2, nb), nb)
+
+        def finish(key, dst):
+            res = sb([P, HALF], F32, f"res{key[0]}{key[1]}")
+            nc.vector.tensor_tensor(res[:], y_banks[key + (1,)][:], gates[key][:], MULT)
+            nc.sync.dma_start(dst, res[:] if key[0] == 2 else res[:].rearrange("p (i m) -> p i m", i=2))
+
+        def finish_early(c, q):
+            rows = out[256 * q : 256 * (q + 1), c * CHUNK : (c + 1) * CHUNK]
+            finish((c, q), rows.rearrange("(i p) m -> p i m", i=2))
 
         for c in range(2):
             for q in range(2):
                 for w in range(2):
-                    second_pass(c, q, w, 0)
+                    early_pass(c, q, w, 0)
         for c in range(2):
             late_gathers(c)
             weave(c)
         quantise_z1(0)
         quantise_z0(1, "xc0")
-        for c in range(CHUNKS):
-            if c + 2 < CHUNKS:
-                late_gathers(c + 2)
-            for q in range(2):
-                products(c, q)
-            if c + 2 < CHUNKS:
-                weave(c + 2)
-            if c >= 1:
-                finish(c - 1, 1)
-            if c + 1 < CHUNKS:
-                quantise_z1(c + 1)
-            finish(c, 0)
-        finish(CHUNKS - 1, 1)
+        for c in range(2):
+            late_gathers(c + 2)
+            if c == 1:
+                weave(3)
+            for w in range(2):
+                for q in range(2):
+                    early_pass(c, q, w, 1)
+            if c == 0:
+                weave(2)
+            if c == 0:
+                quantise_z1(1)
+        for nb in range(4):
+            open_late(nb, 0)
+        for c in range(2, 4):
+            finish_early(0, c - 2)
+            quantise_z1(c)
+            for nb in range(4):
+                add_late(c, nb, 0)
+            open_late(c - 2, 1)
+            add_late(2, c - 2, 1)
+        for nb in range(2):
+            add_late(3, nb, 1)
+        for nb in range(2, 4):
+            finish_early(1, nb - 2)
+            open_late(nb, 1)
+            for c in range(2, 4):
+                add_late(c, nb, 1)
+        for nb in range(4):
+            finish((2, nb), out[nb * P : (nb + 1) * P, HALF:M])

@@ -36,6 +36,7 @@ def tile_list_beam_slot_gating_kernel(
         head = ctx.enter_context(tc.tile_pool(name="head", bufs=1))
         stage = ctx.enter_context(tc.tile_pool(name="stage", bufs=1))
         third = ctx.enter_context(tc.tile_pool(name="third", bufs=1))
+        last = ctx.enter_context(tc.tile_pool(name="last", bufs=1))
         psum = ctx.enter_context(tc.psum_pool(name="psum", bufs=1))
 
         def sb(shape, dtype, name, tag=None):
@@ -107,7 +108,7 @@ def tile_list_beam_slot_gating_kernel(
             nc.vector.tensor_copy(v_w[a][:, lo:hi], tab_w[a][:].indirect(list1[:, lo // 16 : hi // 16]))
 
         w4_s = stage.tile([P, PASSES, H], U8, name="w4_s", offset=0, align_bytes=64)
-        late = stage.tile([P, 17, M], F32, name="late", offset=PASSES * H, align_bytes=64)
+        late = stage.tile([P, 17, M], F32, name="late", offset=PASSES * (H + 4 * N), align_bytes=64)
         wgs_sb = late[:, 16, :]
         nc.sync.dma_start(wgs_sb, wgs)
         ifm_nat = late[:, 0:4, :]
@@ -127,6 +128,14 @@ def tile_list_beam_slot_gating_kernel(
             )
             if k == 0:
                 nc.sync.dma_start(wv_raw, wv.rearrange("(a p j) n -> p a (j n)", a=2, j=4))
+        w8_w = stage.tile([P, PASSES, N], U32, name="w8_w", offset=PASSES * H, align_bytes=64)
+        nc.sync.dma_start(w8_w[:].bitcast(I32), w8_words.rearrange("a p n i -> p a (n i)").bitcast(I32))
+        for q in range(4):
+            nc.sync.dma_start(
+                w4_s[32 * q + 4 : 32 * q + 8, :, 0:N].bitcast(I32),
+                w8_scales[:, 4 * q : 4 * q + 4, :].rearrange("a r n -> r a n").bitcast(I32),
+            )
+
         for g in range(4):
             nc.sync.dma_start(wgs_dealt[32 * g : 32 * (g + 1), :, :], wgs.rearrange("(q t) j -> q t j", t=4))
         ifm_hi = ifm[HALF:H, :].rearrange("(p t) m -> p t m", t=4)
@@ -193,21 +202,20 @@ def tile_list_beam_slot_gating_kernel(
             for dst, lo, hi in pieces:
                 nc.scalar.copy(dst, flat[:, lo:hi])
 
-        w8_w = sb([P, PASSES, N], U32, "w8_w", "v_w0")
-        nc.sync.dma_start(w8_w[:].bitcast(I32), w8_words.rearrange("a p n i -> p a (n i)").bitcast(I32))
-        for q in range(4):
-            nc.sync.dma_start(
-                w4_s[32 * q + 4 : 32 * q + 8, :, 0:N].bitcast(I32),
-                w8_scales[:, 4 * q : 4 * q + 4, :].rearrange("a r n -> r a n").bitcast(I32),
-            )
-
         def scatter(page, values, weights, lo, hi):
             nc.vector.tensor_tensor(page[:].indirect(list2[:, lo // 16 : hi // 16]), values, weights, MULT)
 
         def gather(dst, page, extra, lo, hi):
             nc.vector.tensor_tensor(dst, page[:].indirect(list3[:, lo // 16 : hi // 16]), extra, ADD)
 
-        zt = [sb([P, 2, 2, P, 2], BF16, f"zt{c}") for c in range(CHUNKS)]
+        woven_at = 3 * HALF
+
+        def chunk_tile(shape, dtype, name, c):
+            if c == 1:
+                return last.tile(shape, dtype, name=name, offset=woven_at, align_bytes=64)
+            return sb(shape, dtype, name, f"zt{c}")
+
+        zt = [chunk_tile([P, 2, 2, P, 2], BF16, f"zt{c}", c) for c in range(CHUNKS)]
         z0_in = sb([P, 2 * M], F32, "z0_in")
         hp = {}
         for k in range(2):
@@ -261,16 +269,10 @@ def tile_list_beam_slot_gating_kernel(
         scatter(pages[0], hp[1][:], wgs_dealt[:, 1, :], 0, S)
         x_plane0 = sb([P, M], F32, "x_plane0", "x0")
         gather(x_plane0[:], pages[2], ifm_dealt[:, 0, :], 0, M)
-        z1_in = [sb([P, CHUNK, 4], BF16, f"z1_in{c}", f"zt{c}") for c in range(CHUNKS)]
+        z1_in = [chunk_tile([P, CHUNK, 4], BF16, f"z1_in{c}", c) for c in range(CHUNKS)]
         for c in range(CHUNKS):
             nc.scalar.copy(z1_in[c][:, :, 0], x_plane0[:, c * CHUNK : (c + 1) * CHUNK])
 
-        hp[2] = sb([P, S], F32, "hp2", "wv_bf")
-        hp[3] = sb([P, S], F32, "hp3", "h2")
-        for t in range(2, 4):
-            for jh in range(2):
-                turn_plane(t, jh, [(hp[t][:, jh * HALF : (jh + 1) * HALF], 0, HALF)])
-            scatter(pages[t - 1], hp[t][:], wgs_dealt[:, t, :], 0, S)
         z0 = {}
 
         def quantise_z0(half, tag):
@@ -281,7 +283,14 @@ def tile_list_beam_slot_gating_kernel(
             )
             z0[half] = (z0_w, z0_s)
 
-        quantise_z0(0, "wv_bf")
+        hp[2] = sb([P, S], F32, "hp2", "wv_bf")
+        hp[3] = sb([P, S], F32, "hp3", "h2")
+        for t in range(2, 4):
+            for jh in range(2):
+                turn_plane(t, jh, [(hp[t][:, jh * HALF : (jh + 1) * HALF], 0, HALF)])
+        quantise_z0(0, "h1")
+        for t in range(2, 4):
+            scatter(pages[t - 1], hp[t][:], wgs_dealt[:, t, :], 0, S)
 
         z1 = {}
         xc = {}
@@ -290,7 +299,10 @@ def tile_list_beam_slot_gating_kernel(
 
         def late_gathers(c):
             cols = slice(c * CHUNK, (c + 1) * CHUNK)
-            xc[c] = sb([P, 3, CHUNK], F32, f"xc{c}", ("xc0", "xc1", "zt0", "xc1")[c])
+            if c == 3:
+                xc[c] = chunk_tile([P, 3, CHUNK], F32, "xc3", 1)
+            else:
+                xc[c] = sb([P, 3, CHUNK], F32, f"xc{c}", f"xc{c % 2}")
             for i in range(3):
                 gather(xc[c][:, i, :], pages[i], ifm_dealt[:, 1 + i, cols], c * CHUNK, (c + 1) * CHUNK)
 
@@ -348,7 +360,11 @@ def tile_list_beam_slot_gating_kernel(
                 sigmoid((2, nb), nb)
 
         def finish(key, dst):
-            res = sb([P, HALF], F32, f"res{key[0]}{key[1]}")
+            if key[0] < 2 and key != (0, 0):
+                slot = 2 * key[0] + key[1] - 1
+                res = last.tile([P, HALF], F32, name=f"res{key[0]}{key[1]}", offset=4 * HALF * slot, align_bytes=64)
+            else:
+                res = sb([P, HALF], F32, f"res{key[0]}{key[1]}")
             nc.vector.tensor_tensor(res[:], y_banks[key + (1,)][:], gates[key][:], MULT)
             nc.sync.dma_start(dst, res[:] if key[0] == 2 else res[:].rearrange("p (i m) -> p i m", i=2))
 
@@ -364,31 +380,29 @@ def tile_list_beam_slot_gating_kernel(
             late_gathers(c)
             weave(c)
         quantise_z1(0)
-        quantise_z0(1, "xc0")
         for c in range(2):
             late_gathers(c + 2)
-            if c == 1:
-                weave(3)
             for w in range(2):
                 for q in range(2):
                     early_pass(c, q, w, 1)
-            if c == 0:
-                weave(2)
+            weave(c + 2)
             if c == 0:
                 quantise_z1(1)
+                quantise_z0(1, "xc1")
         for nb in range(4):
             open_late(nb, 0)
-        for c in range(2, 4):
-            finish_early(0, c - 2)
-            quantise_z1(c)
-            for nb in range(4):
-                add_late(c, nb, 0)
-            open_late(c - 2, 1)
-            add_late(2, c - 2, 1)
-        for nb in range(2):
-            add_late(3, nb, 1)
-        for nb in range(2, 4):
-            finish_early(1, nb - 2)
+        quantise_z1(2)
+        for nb in range(4):
+            add_late(2, nb, 0)
+        finish_early(0, 0)
+        open_late(0, 1)
+        add_late(2, 0, 1)
+        quantise_z1(3)
+        for nb in range(4):
+            add_late(3, nb, 0)
+        add_late(3, 0, 1)
+        for nb in range(1, 4):
+            finish_early(nb // 2, nb % 2)
             open_late(nb, 1)
             for c in range(2, 4):
                 add_late(c, nb, 1)

@@ -108,7 +108,7 @@ def tile_list_beam_slot_gating_kernel(
             nc.vector.tensor_copy(v_w[a][:, lo:hi], tab_w[a][:].indirect(list1[:, lo // 16 : hi // 16]))
 
         w4_s = stage.tile([P, PASSES, H], U8, name="w4_s", offset=0, align_bytes=64)
-        late = stage.tile([P, 17, M], F32, name="late", offset=PASSES * (H + 4 * N), align_bytes=64)
+        late = stage.tile([P, 17, M], F32, name="late", offset=PASSES * (H + 5 * N), align_bytes=64)
         wgs_sb = late[:, 16, :]
         nc.sync.dma_start(wgs_sb, wgs)
         ifm_nat = late[:, 0:4, :]
@@ -130,9 +130,10 @@ def tile_list_beam_slot_gating_kernel(
                 nc.sync.dma_start(wv_raw, wv.rearrange("(a p j) n -> p a (j n)", a=2, j=4))
         w8_w = stage.tile([P, PASSES, N], U32, name="w8_w", offset=PASSES * H, align_bytes=64)
         nc.sync.dma_start(w8_w[:].bitcast(I32), w8_words.rearrange("a p n i -> p a (n i)").bitcast(I32))
+        w8_s = stage.tile([P, PASSES, N], U8, name="w8_s", offset=PASSES * (H + 4 * N), align_bytes=64)
         for q in range(4):
             nc.sync.dma_start(
-                w4_s[32 * q + 4 : 32 * q + 8, :, 0:N].bitcast(I32),
+                w8_s[32 * q : 32 * q + 4, :, :].bitcast(I32),
                 w8_scales[:, 4 * q : 4 * q + 4, :].rearrange("a r n -> r a n").bitcast(I32),
             )
 
@@ -298,19 +299,24 @@ def tile_list_beam_slot_gating_kernel(
         y_banks = {}
 
         def late_gathers(c):
-            cols = slice(c * CHUNK, (c + 1) * CHUNK)
             if c == 3:
                 xc[c] = chunk_tile([P, 3, CHUNK], F32, "xc3", 1)
             else:
                 xc[c] = sb([P, 3, CHUNK], F32, f"xc{c}", f"xc{c % 2}")
             for i in range(3):
-                gather(xc[c][:, i, :], pages[i], ifm_dealt[:, 1 + i, cols], c * CHUNK, (c + 1) * CHUNK)
+                for lo, hi in pieces(c) if i == 2 else [(0, CHUNK)]:
+                    m0, m1 = c * CHUNK + lo, c * CHUNK + hi
+                    gather(xc[c][:, i, lo:hi], pages[i], ifm_dealt[:, 1 + i, m0:m1], m0, m1)
+
+        def pieces(c):
+            return [(0, P), (P, CHUNK)] if c == CHUNKS - 1 else [(0, CHUNK)]
 
         def weave(c):
-            nc.scalar.copy(
-                z1_in[c][:, :, 1:4].rearrange("p (g i) t -> p g t i", i=4),
-                xc[c][:].rearrange("p t (g i) -> p g t i", i=4),
-            )
+            for lo, hi in pieces(c):
+                nc.scalar.copy(
+                    z1_in[c][:, lo:hi, 1:4].rearrange("p (g i) t -> p g t i", i=4),
+                    xc[c][:, :, lo:hi].rearrange("p t (g i) -> p g t i", i=4),
+                )
 
         def quantise_z1(c):
             z1_w = sb([P, CHUNK], U32, f"z1_w{c}")
@@ -321,11 +327,11 @@ def tile_list_beam_slot_gating_kernel(
             z1[c] = (z1_w, z1_s)
 
         def mx_pass(dst, nb, w, a, z_w, z_s, start, stop):
-            w_w, w_s, row = ((w8_w, w4_s, 4), (wv_w, wv_s, 0))[w]
+            w_w, w_s = ((w8_w, w8_s), (wv_w, wv_s))[w]
             nc.tensor.matmul_mx(
                 out=dst,
                 lhsT=w_w[:, a, nb * P : (nb + 1) * P].bitcast(FP8X4),
-                lhsT_scale=w_s[row:P, a, nb * P : (nb + 1) * P],
+                lhsT_scale=w_s[:, a, nb * P : (nb + 1) * P],
                 rhs=z_w.bitcast(FP8X4),
                 rhs_scale=z_s,
                 start=start,

from contextlib import ExitStack

import concourse.mybir as mybir
from concourse.masks import make_identity

T, S, K, H, T2, M, N = 2048, 1024, 1024, 1024, 2048, 1024, 512
FLOPS = 2 * K * H * S + 2 * 2 * H * N * M

F32 = mybir.dt.float32
BF16 = mybir.dt.bfloat16
I32 = mybir.dt.int32
U32 = mybir.dt.uint32
U16 = mybir.dt.uint16
U8 = mybir.dt.uint8
FP8X4 = mybir.dt.float8_e4m3fn_x4
FP4X4 = mybir.dt.float4_e2m1fn_x4
MULT = mybir.AluOpType.mult
ADD = mybir.AluOpType.add
SIGMOID = mybir.ActivationFunctionType.Sigmoid

P = 128
PASSES = 2
HALF = 512
CHUNK = 256
CHUNKS = M // CHUNK
FIRST = 2
LEAD = 256


def tile_list_beam_slot_gating_kernel(
    tc, tab_words, tab_scales, offs, w4_words, w4_scales, wgs, offs2, offs3, ifm, wv, w8_words, w8_scales, out
):
    nc = tc.nc
    with ExitStack() as ctx:
        keep = ctx.enter_context(tc.tile_pool(name="keep", bufs=1))
        head = ctx.enter_context(tc.tile_pool(name="head", bufs=1))
        stage = ctx.enter_context(tc.tile_pool(name="stage", bufs=1))
        third = ctx.enter_context(tc.tile_pool(name="third", bufs=1))
        last = ctx.enter_context(tc.tile_pool(name="last", bufs=1))
        psum = ctx.enter_context(tc.psum_pool(name="psum", bufs=1))

        def sb(shape, dtype, name, tag=None):
            return keep.tile(shape, dtype, name=name, tag=tag or name, align_bytes=64)

        def bank_tile(shape, name, index):
            return psum.tile(shape, F32, name=name, tag=f"bank{index}")

        list1 = keep.tile([P, S // 16], U16, name="list1")
        list2 = keep.tile([P, S // 16], U16, name="list2")
        list3 = keep.tile([P, M // 16], U16, name="list3")
        nc.sync.dma_start(list1[:], offs)

        tab_s = head.tile([P, T], U8, name="tab_s", offset=0, align_bytes=64)
        nc.sync.dma_start(tab_s[0:32, :].bitcast(I32), tab_scales.rearrange("a q t -> q a t").bitcast(I32))
        nc.vector.memset(tab_s[32:64, :].bitcast(I32), 0)
        nc.vector.memset(tab_s[64:P, :].bitcast(I32), 0)

        w4_s_first = sb([P, PASSES, P * FIRST], U8, "w4_s_first")
        nc.gpsimd.memset(w4_s_first[:].rearrange("p a n -> p (a n)").bitcast(I32), 0)
        tab_w = []
        for a in range(PASSES):
            if a == 0:
                t = stage.tile([P, T], U32, name="tab_w0", offset=0, align_bytes=64)
            else:
                t = sb([P, T], U32, "tab_w1", "big1")
            nc.sync.dma_start(t[:].bitcast(I32), tab_words[a].rearrange("p t i -> p (t i)").bitcast(I32))
            tab_w.append(t)
        w4_hbm = w4_words.rearrange("a p n -> p a n")
        w4_first = third.tile([P, PASSES, 2 * P * FIRST], U8, name="w4_first", offset=0, align_bytes=64)
        nc.sync.dma_start(w4_first[:].bitcast(I32), w4_hbm[:, :, 0 : 2 * P * FIRST].bitcast(I32))
        nc.sync.dma_start(list2[:], offs2)
        nc.sync.dma_start(list3[:], offs3)
        v_planes = sb([P, PASSES, S], U8, "v_planes")
        nc.vector.memset(v_planes[:].rearrange("p a n -> p (a n)").bitcast(I32), 0)
        for q in range(4):
            nc.gpsimd.dma_start(
                w4_s_first[32 * q : 32 * q + 4, :, :].bitcast(I32),
                w4_scales[:, 4 * q : 4 * q + 4, 0 : P * FIRST].rearrange("a r n -> r a n").bitcast(I32),
            )

        pages = [sb([P, T2], F32, "page0")]
        nc.vector.memset(pages[0][:].bitcast(I32), 0)

        warm = sb([P, 8], F32, "warm")
        nc.vector.memset(warm[:], 0.0)
        nc.scalar.activation(warm[:, 1:2], warm[:, 0:1], SIGMOID)


        v_rows = sb([P, S], U8, "v_rows")
        for lo, hi in ((0, LEAD), (LEAD, S)):
            nc.vector.tensor_copy(v_rows[:, lo:hi], tab_s[:].indirect(list1[:, lo // 16 : hi // 16]))
            for q in range(4):
                nc.scalar.dma_start(
                    v_planes[32 * q : 32 * q + 4, :, lo:hi].bitcast(I32),
                    v_rows[8 * q : 8 * q + 8, lo:hi].bitcast(I32),
                )
        v_s = [v_planes[:, a, :] for a in range(PASSES)]
        wgs_lead = head.tile([P, LEAD], F32, name="wgs_lead", offset=0, align_bytes=64)
        nc.sync.dma_start(wgs_lead[:], wgs[:, 0:LEAD])
        pages.append(head.tile([P, T2], F32, name="page1", offset=4 * LEAD + 4 * P, align_bytes=64))
        nc.gpsimd.memset(pages[1][:].bitcast(I32), 0)
        ident = head.tile([P, P], F32, name="ident", offset=4 * LEAD, align_bytes=64)
        make_identity(nc, ident[:])


        v_w = [sb([P, S], U32, f"v_w{a}") for a in range(PASSES)]
        for a, lo, hi in ((0, 0, S), (1, 0, LEAD), (1, LEAD, S)):
            nc.vector.tensor_copy(v_w[a][:, lo:hi], tab_w[a][:].indirect(list1[:, lo // 16 : hi // 16]))

        w4_s = stage.tile([P, PASSES, H], U8, name="w4_s", offset=0, align_bytes=64)
        late = stage.tile([P, 17, M], F32, name="late", offset=PASSES * (H + 5 * N), align_bytes=64)
        wgs_sb = late[:, 16, :]
        nc.sync.dma_start(wgs_sb, wgs)
        ifm_nat = late[:, 0:4, :]
        ifm_dealt = late[:, 4:8, :]
        wgs_dealt = late[:, 8:12, :]
        wv_raw = late[:, 12:16, :].rearrange("p (a x) m -> p a (x m)", a=2)
        w4_rest = sb([P, PASSES, 2 * (H - P * FIRST)], U8, "w4_rest", "v_rows")
        nc.sync.dma_start(w4_rest[:].bitcast(I32), w4_hbm[:, :, 2 * P * FIRST : 2 * H].bitcast(I32))
        for q in range(4):
            nc.sync.dma_start(
                w4_s[32 * q : 32 * q + 4, :, P * FIRST : H].bitcast(I32),
                w4_scales[:, 4 * q : 4 * q + 4, P * FIRST : H].rearrange("a r n -> r a n").bitcast(I32),
            )
        for k in range(2):
            nc.sync.dma_start(
                ifm_nat[:, 2 * k : 2 * k + 2, :], ifm[256 * k : 256 * (k + 1), :].rearrange("(s p) m -> p s m", s=2)
            )
            if k == 0:
                nc.sync.dma_start(wv_raw, wv.rearrange("(a p j) n -> p a (j n)", a=2, j=4))
        w8_w = stage.tile([P, PASSES, N], U32, name="w8_w", offset=PASSES * H, align_bytes=64)
        nc.sync.dma_start(w8_w[:].bitcast(I32), w8_words.rearrange("a p n i -> p a (n i)").bitcast(I32))
        w8_s = stage.tile([P, PASSES, N], U8, name="w8_s", offset=PASSES * (H + 4 * N), align_bytes=64)
        for q in range(4):
            nc.sync.dma_start(
                w8_s[32 * q : 32 * q + 4, :, :].bitcast(I32),
                w8_scales[:, 4 * q : 4 * q + 4, :].rearrange("a r n -> r a n").bitcast(I32),
            )

        for g in range(4):
            nc.sync.dma_start(wgs_dealt[32 * g : 32 * (g + 1), :, :], wgs.rearrange("(q t) j -> q t j", t=4))
        ifm_hi = ifm[HALF:H, :].rearrange("(p t) m -> p t m", t=4)
        for u in range(2):
            nc.sync.dma_start(ifm_dealt[:, 2 * u : 2 * u + 2, :], ifm_hi[:, 2 * u : 2 * u + 2, :])

        h = [sb([P, S], F32, f"h{s}") for s in range(4)]

        def first_product(s, lo, hi, index):
            bank = bank_tile([P, hi - lo], f"h_bank{s}_{lo}", index)
            w4 = w4_first if s < FIRST else w4_rest
            c0 = 2 * P * (s if s < FIRST else s - FIRST)
            width = HALF if hi - lo == HALF else P
            for a in range(PASSES):
                for j0 in range(lo, hi, width):
                    nc.tensor.matmul_mx(
                        out=bank[:, j0 - lo : j0 - lo + width],
                        lhsT=w4[:, a, c0 : c0 + 2 * P].bitcast(FP4X4),
                        lhsT_scale=(w4_s_first if s < FIRST else w4_s)[:, a, s * P : (s + 1) * P],
                        rhs=v_w[a][:, j0 : j0 + width].bitcast(FP8X4),
                        rhs_scale=v_s[a][:, j0 : j0 + width],
                        start=(a == 0 and j0 == lo),
                        stop=(a == PASSES - 1 and j0 + width == hi),
                    )
            nc.scalar.copy(h[s][:, lo:hi], bank[:])

        for s in range(2):
            first_product(s, 0, LEAD, s)
        for s in range(2):
            first_product(s, LEAD, LEAD + HALF, 0)
            first_product(s, LEAD + HALF, S, 1)
        for s in range(2, 4):
            for jh in range(2):
                first_product(s, jh * HALF, (jh + 1) * HALF, 2 * jh + s % 2)

        h_t = [sb([P, 4, 4, P], F32, f"h_t{jh}", ("h_t0", "big1")[jh]) for jh in range(2)]
        c_hi = 2 * (HALF - P * FIRST)
        for jh in range(2):
            for i in range(4):
                bank = bank_tile([P, HALF], f"ht_bank{jh}{i}", 4 + i)
                j0 = jh * HALF + i * P
                for a in range(PASSES):
                    nc.tensor.matmul_mx(
                        out=bank[:],
                        lhsT=v_w[a][:, j0 : j0 + P].bitcast(FP8X4),
                        lhsT_scale=v_s[a][:, j0 : j0 + P],
                        rhs=w4_rest[:, a, c_hi : c_hi + 2 * HALF].bitcast(FP4X4),
                        rhs_scale=w4_s[:, a, HALF:H],
                        start=(a == 0),
                        stop=(a == PASSES - 1),
                    )
                nc.scalar.copy(h_t[jh][:, i, :, :], bank[:].rearrange("j (q t) -> j t q", t=4))

        wv_tile = sb([P, 4 * M], BF16, "wv_bf")
        wv_bf = wv_tile[:].rearrange("p (a n j) -> p a n j", a=2, j=4)
        for a in range(PASSES):
            nc.scalar.copy(wv_bf[:, a, :, :], wv_raw[:, a, :].rearrange("p (j n) -> p n j", j=4))

        def turn_plane(t, jh, pieces):
            bank = bank_tile([P, 4, P], f"plane_bank{t}{jh}", 2 * jh + t % 2)
            for i in range(4):
                nc.tensor.transpose(bank[:, i, :], h_t[jh][:, i, t, :], ident[:])
            flat = bank[:].rearrange("p i j -> p (i j)")
            for dst, lo, hi in pieces:
                nc.scalar.copy(dst, flat[:, lo:hi])

        def scatter(page, values, weights, lo, hi):
            nc.vector.tensor_tensor(page[:].indirect(list2[:, lo // 16 : hi // 16]), values, weights, MULT)

        def gather(dst, page, extra, lo, hi):
            nc.vector.tensor_tensor(dst, page[:].indirect(list3[:, lo // 16 : hi // 16]), extra, ADD)

        woven_at = 3 * HALF

        def chunk_tile(shape, dtype, name, c):
            if c == 1:
                return last.tile(shape, dtype, name=name, offset=woven_at, align_bytes=64)
            return sb(shape, dtype, name, f"zt{c}")

        zt = [chunk_tile([P, 2, 2, P, 2], BF16, f"zt{c}", c) for c in range(CHUNKS)]
        z0_in = sb([P, 2 * M], F32, "z0_in")
        hp = {}
        for k in range(2):
            if k == 0:
                for i in range(2):
                    scatter(pages[i], h[i][:, 0:LEAD], wgs_lead[:], 0, LEAD)
                for i in range(2):
                    scatter(pages[i], h[i][:, LEAD:S], wgs_sb[:, LEAD:S], LEAD, S)
            else:
                for i in range(2):
                    scatter(pages[i], h[2 + i][:], wgs_sb, 0, S)
            x = sb([P, 2, M], F32, f"x{k}")
            for i in range(2):
                gather(x[:, i, :], pages[i], ifm_nat[:, 2 * k + i, :], 0, M)
            if k == 0:
                for t in range(2):
                    hp[t] = sb([P, S], F32, f"hp{t}", f"h{t}")
                    for jh in range(2):
                        turn_plane(t, jh, [(hp[t][:, jh * HALF : (jh + 1) * HALF], 0, HALF)])
            for c in range(CHUNKS):
                bank = bank_tile([P, 2, 2, P], f"A{k}{c}", 4 + c)
                for i in range(2):
                    for b in range(2):
                        m0 = c * CHUNK + b * P
                        nc.tensor.transpose(bank[:, b, i, :], x[:, i, m0 : m0 + P], ident[:])
                nc.scalar.copy(
                    zt[c][:, :, :, 64 * k : 64 * (k + 1), :],
                    bank[:].rearrange("m b i r -> m b (i r)").rearrange("m b (p u e) -> m b u p e", u=2, e=2),
                )
        for c in range(CHUNKS):
            bank = bank_tile([P, 2, 2, P], f"B{c}", c)
            words = zt[c][:].rearrange("m b u p e -> m (b u p e)").bitcast(F32)
            for b in range(2):
                for u in range(2):
                    w0 = (2 * b + u) * P
                    nc.tensor.transpose(bank[:, b, u, :], words[:, w0 : w0 + P], ident[:])
            dst = z0_in[:, 2 * c * CHUNK : 2 * (c + 1) * CHUNK]
            nc.scalar.copy(dst.rearrange("p (b m u) -> p b m u", b=2, u=2), bank[:].rearrange("p b u m -> p b m u"))

        wv_s = sb([P, PASSES, N], U8, "wv_s")
        wv_w = sb([P, PASSES, N], U32, "wv_w")
        nc.vector.quantize_mx(
            out=wv_w[:].rearrange("p a n -> p (a n)").bitcast(FP8X4),
            scales=wv_s[:].rearrange("p a n -> p (a n)"),
            in_=wv_tile[:],
        )

        pages.append(third.tile([P, T2], F32, name="page2", offset=0, align_bytes=64))
        nc.gpsimd.memset(pages[2][:].bitcast(I32), 0)
        scatter(pages[2], hp[0][:], wgs_dealt[:, 0, :], 0, S)
        scatter(pages[0], hp[1][:], wgs_dealt[:, 1, :], 0, S)
        x_plane0 = sb([P, M], F32, "x_plane0", "x0")
        gather(x_plane0[:], pages[2], ifm_dealt[:, 0, :], 0, M)
        z1_in = [chunk_tile([P, CHUNK, 4], BF16, f"z1_in{c}", c) for c in range(CHUNKS)]
        for c in range(CHUNKS):
            nc.scalar.copy(z1_in[c][:, :, 0], x_plane0[:, c * CHUNK : (c + 1) * CHUNK])

        z0 = {}

        def quantise_z0(half, tag):
            z0_w = sb([P, HALF], U32, f"z0_w{half}", tag)
            z0_s = sb([P, HALF], U8, f"z0_s{half}")
            nc.vector.quantize_mx(
                out=z0_w[:].bitcast(FP8X4), scales=z0_s[:], in_=z0_in[:, half * M : (half + 1) * M].bitcast(BF16)
            )
            z0[half] = (z0_w, z0_s)

        hp[2] = sb([P, S], F32, "hp2", "wv_bf")
        hp[3] = sb([P, S], F32, "hp3", "h2")
        for t in range(2, 4):
            for jh in range(2):
                turn_plane(t, jh, [(hp[t][:, jh * HALF : (jh + 1) * HALF], 0, HALF)])
        quantise_z0(0, "h1")
        for t in range(2, 4):
            scatter(pages[t - 1], hp[t][:], wgs_dealt[:, t, :], 0, S)

        z1 = {}
        xc = {}
        gates = {}
        y_banks = {}

        def late_gathers(c):
            if c == 3:
                xc[c] = chunk_tile([P, 3, CHUNK], F32, "xc3", 1)
            else:
                xc[c] = sb([P, 3, CHUNK], F32, f"xc{c}", f"xc{c % 2}")
            for i in range(3):
                for lo, hi in pieces(c) if i == 2 else [(0, CHUNK)]:
                    m0, m1 = c * CHUNK + lo, c * CHUNK + hi
                    gather(xc[c][:, i, lo:hi], pages[i], ifm_dealt[:, 1 + i, m0:m1], m0, m1)

        def pieces(c):
            return [(0, P), (P, CHUNK)] if c == CHUNKS - 1 else [(0, CHUNK)]

        def weave(c):
            for lo, hi in pieces(c):
                nc.scalar.copy(
                    z1_in[c][:, lo:hi, 1:4].rearrange("p (g i) t -> p g t i", i=4),
                    xc[c][:, :, lo:hi].rearrange("p t (g i) -> p g t i", i=4),
                )

        def quantise_z1(c):
            z1_w = sb([P, CHUNK], U32, f"z1_w{c}")
            z1_s = sb([P, CHUNK], U8, f"z1_s{c}")
            nc.vector.quantize_mx(
                out=z1_w[:].bitcast(FP8X4), scales=z1_s[:], in_=z1_in[c][:].rearrange("p m t -> p (m t)")
            )
            z1[c] = (z1_w, z1_s)

        def mx_pass(dst, nb, w, a, z_w, z_s, start, stop):
            w_w, w_s = ((w8_w, w8_s), (wv_w, wv_s))[w]
            nc.tensor.matmul_mx(
                out=dst,
                lhsT=w_w[:, a, nb * P : (nb + 1) * P].bitcast(FP8X4),
                lhsT_scale=w_s[:, a, nb * P : (nb + 1) * P],
                rhs=z_w.bitcast(FP8X4),
                rhs_scale=z_s,
                start=start,
                stop=stop,
            )

        def sigmoid(key, slot):
            gates[key] = sb([P, HALF], F32, f"gate{key[0]}{key[1]}", f"gate{slot}")
            nc.scalar.activation(gates[key][:], y_banks[key + (0,)][:], SIGMOID)

        def early_pass(c, q, w, a):
            if a == 0:
                y_banks[(c, q, w)] = bank_tile([P, HALF], f"Y{c}{q}{w}", 4 * c + 2 * q + w)
                part = slice(c * CHUNK, (c + 1) * CHUNK)
                z_w, z_s = z0[0][0][:, part], z0[0][1][:, part]
            else:
                z_w, z_s = z1[c][0][:], z1[c][1][:]
            for i in range(2):
                dst = y_banks[(c, q, w)][:, i * CHUNK : (i + 1) * CHUNK]
                mx_pass(dst, 2 * q + i, w, a, z_w, z_s, a == 0 and i == 0, a == 1 and i == 1)
            if a == 1 and w == 0:
                sigmoid((c, q), 2 * c + q)

        def open_late(nb, w):
            y_banks[(2, nb, w)] = bank_tile([P, HALF], f"Y2{nb}{w}", 2 * nb + w)
            mx_pass(y_banks[(2, nb, w)][:], nb, w, 0, z0[1][0][:], z0[1][1][:], True, False)

        def add_late(c, nb, w):
            dst = y_banks[(2, nb, w)][:, (c - 2) * CHUNK : (c - 1) * CHUNK]
            mx_pass(dst, nb, w, 1, z1[c][0][:], z1[c][1][:], False, c == 3)
            if c == 3 and w == 0:
                sigmoid((2, nb), nb)

        def finish(key, dst):
            if key[0] < 2 and key != (0, 0):
                slot = 2 * key[0] + key[1] - 1
                res = last.tile([P, HALF], F32, name=f"res{key[0]}{key[1]}", offset=4 * HALF * slot, align_bytes=64)
            else:
                res = sb([P, HALF], F32, f"res{key[0]}{key[1]}")
            nc.vector.tensor_tensor(res[:], y_banks[key + (1,)][:], gates[key][:], MULT)
            nc.sync.dma_start(dst, res[:] if key[0] == 2 else res[:].rearrange("p (i m) -> p i m", i=2))

        def finish_early(c, q):
            rows = out[256 * q : 256 * (q + 1), c * CHUNK : (c + 1) * CHUNK]
            finish((c, q), rows.rearrange("(i p) m -> p i m", i=2))

        for c in range(2):
            for q in range(2):
                for w in range(2):
                    early_pass(c, q, w, 0)
        for c in range(2):
            late_gathers(c)
            weave(c)
        quantise_z1(0)
        for c in range(2):
            late_gathers(c + 2)
            for w in range(2):
                for q in range(2):
                    early_pass(c, q, w, 1)
            weave(c + 2)
            if c == 0:
                quantise_z1(1)
                quantise_z0(1, "xc1")
        for nb in range(4):
            open_late(nb, 0)
        quantise_z1(2)
        for nb in range(4):
            add_late(2, nb, 0)
        finish_early(0, 0)
        open_late(0, 1)
        add_late(2, 0, 1)
        quantise_z1(3)
        for nb in range(4):
            add_late(3, nb, 0)
        add_late(3, 0, 1)
        for nb in range(1, 4):
            finish_early(nb // 2, nb % 2)
            open_late(nb, 1)
            for c in range(2, 4):
                add_late(c, nb, 1)
        for nb in range(4):
            finish((2, nb), out[nb * P : (nb + 1) * P, HALF:M])
